import numpy as np
import ml_dtypes


def mxq(x, axis, fmt="e4m3"):
    dtype, down = {"e4m3": (ml_dtypes.float8_e4m3fn, 7), "e5m2": (ml_dtypes.float8_e5m2, 14)}[fmt]
    v = np.moveaxis(np.asarray(x, np.float32).astype(ml_dtypes.bfloat16).astype(np.float64), axis, -1)
    blocks = v.reshape(v.shape[:-1] + (-1, 32))
    amax = np.abs(blocks).max(-1, keepdims=True)
    byte = np.maximum(np.where(amax > 0, np.frexp(amax)[1] - 1 + 127, 0) - down, 1)
    scale = np.exp2(byte - 127.0)
    codes = (blocks / scale).astype(np.float32).astype(dtype).astype(np.float64)
    return np.moveaxis((codes * scale).reshape(v.shape), -1, axis)


WIDE = False


def mx_kscale(k):
    if not WIDE:
        return np.ones(k)
    levels = np.array([10, -10, 5, -5, 0])
    if k % 512:
        return np.exp2(np.random.permutation(np.resize(levels, k // 32))).repeat(32)
    a = np.empty((k // 512, 16))
    for p in range(k // 512):
        a[p, :8] = np.random.permutation(np.resize(levels, 8))
        for g in range(8):
            far = levels[np.abs(levels - a[p, g]) >= 10]
            a[p, g + 8] = far[np.random.randint(len(far))]
    return np.exp2(a.ravel()).repeat(32)


BF16 = ml_dtypes.bfloat16


def bf(x):
    return np.asarray(x, np.float32).astype(BF16)


def f64(x):
    return np.asarray(x).astype(np.float64)


B, L, D, E = 256, 4, 512, 1024


def erf(a):
    c = np.clip(a, -6.0, 6.0)
    c2 = c * c
    term = c
    total = c
    for n in range(1, 150):
        term = term * (2.0 * c2 / (2.0 * n + 1.0))
        total = total + term
    v = 2.0 / np.sqrt(np.pi) * np.exp(-c2) * total
    return np.where(np.abs(a) <= 6.0, v, np.sign(a))


def gelu_erf(v):
    return 0.5 * v * (1.0 + erf(v / np.sqrt(2.0)))


def softplus(r):
    return np.maximum(r, 0.0) + np.log(1.0 + np.exp(-np.abs(r)))


def draw0():
    s1, s2 = mx_kscale(D), mx_kscale(D)
    t = mx_kscale(E)
    c = 1.0 / np.sqrt(D)
    return {
        "x": bf(np.random.standard_normal((B, L, D)) * s1),
        "y": bf(np.random.standard_normal((B, D)) * s2),
        "wu": bf(np.random.standard_normal((D, E)) * c / s1[:, None] * t[None, :]),
        "bu": bf(np.random.standard_normal(E) * 0.3 * t),
        "wg": bf(np.random.standard_normal((D, E)) * c / s2[:, None]),
        "bg": bf(np.random.standard_normal(E) * 0.3),
        "gain": bf((1.0 + 0.1 * np.random.standard_normal(E)) / t),
    }


def core(x, y, wu, bu, wg, bg, gain):
    n, patches, _ = x.shape
    u = (mxq(f64(x), 2, "e4m3") @ mxq(f64(wu), 0, "e4m3")) + f64(bu)
    g = f64(gain) * gelu_erf((mxq(f64(y), 1, "e4m3") @ mxq(f64(wg), 0, "e4m3")) + f64(bg))
    u_flat = u.reshape(n * patches, u.shape[-1])
    s = (mxq(g, 1, "e4m3") @ mxq(u_flat, 1, "e4m3").T) / 16.0
    s = s.reshape(n, n, patches)
    idx = np.arange(n)
    positive = (idx[:, None] == idx[None, :])[:, :, None]
    r = np.where(positive, -s, s)
    return softplus(r)


def e4m3fn_bytes(y):
    return np.clip(np.asarray(y, np.float64), -448.0, 448.0).astype(np.float32).astype(ml_dtypes.float8_e4m3fn).view(np.uint8)


def e4m3fn_values(b):
    return np.asarray(b, np.uint8).view(ml_dtypes.float8_e4m3fn).astype(np.float64)


def setup_inputs():
    d = draw0()
    x0 = np.asarray(d['x']).astype(np.float64)
    s = (np.max(np.abs(x0), axis=(0, 1), keepdims=True) / 448.0).astype(np.float32)
    out = {}
    for k, v in d.items():
        if k == 'x':
            out['x_bytes'] = e4m3fn_bytes(x0 / s.astype(np.float64))
            out['x_scale'] = s
        else:
            out[k] = v
    return out


def reference(x_bytes, x_scale, y, wu, bu, wg, bg, gain):
    return core(e4m3fn_values(x_bytes) * x_scale.astype(np.float64), y, wu, bu, wg, bg, gain)

@@ -1,0 +1,318 @@
+from contextlib import ExitStack
+
+import concourse.mybir as mybir
+from concourse.masks import make_identity
+
+B, L, D, E = 256, 4, 512, 1024
+FLOPS = 2 * (B * L * D * E + B * D * E + B * B * L * E)
+
+F32 = mybir.dt.float32
+BF16 = mybir.dt.bfloat16
+U32 = mybir.dt.uint32
+U8 = mybir.dt.uint8
+FP8 = mybir.dt.float8_e4m3fn
+FP8X4 = mybir.dt.float8_e4m3fn_x4
+ALU = mybir.AluOpType
+ACT = mybir.ActivationFunctionType
+
+P = 128
+PACK = 4
+HALF = 512
+SCORE_SCALE = 1.0 / 16.0
+EXP_CAP = 2.0 ** 60
+
+
+def tile_deepinfomaxlocalglobaljsdmap_kernel(tc, x_bytes, x_scale, y, wu, bu, wg, bg, gain, out):
+    nc = tc.nc
+    with ExitStack() as ctx:
+        sb = ctx.enter_context(tc.tile_pool(name="sb", bufs=1))
+        turn = ctx.enter_context(tc.psum_pool(name="turn", bufs=2))
+        mm = ctx.enter_context(tc.psum_pool(name="mm", bufs=4))
+        score = ctx.enter_context(tc.psum_pool(name="score", bufs=2))
+        ctx.enter_context(tc.manual_schedule())
+
+        def new(name, shape, dtype):
+            return sb.tile(shape, dtype, name=name, align_bytes=64)
+
+        def quantize(name, grouped):
+            width = grouped.shape[1] // PACK
+            codes = new(name + "_codes", [P, width], U32)
+            scales = new(name + "_scales", [P, width], U8)
+            nc.vector.quantize_mx(out=codes[:].bitcast(FP8X4), scales=scales[:], in_=grouped[:])
+            return codes, scales
+
+        def matmul(acc, stationary, m0, moving, n0, n, start=True, stop=True):
+            nc.tensor.matmul_mx(
+                out=acc,
+                lhsT=stationary[0][:, m0 : m0 + P].bitcast(FP8X4),
+                lhsT_scale=stationary[1][:, m0 : m0 + P],
+                rhs=moving[0][:, n0 : n0 + n].bitcast(FP8X4),
+                rhs_scale=moving[1][:, n0 : n0 + n],
+                start=start,
+                stop=stop,
+            )
+
+        rows = new("rows", [P, 2 * P], BF16)
+        nc.vector.memset(rows[:], 0.0)
+        ident = new("ident", [P, P], F32)
+        make_identity(nc, ident[:])
+        ident_bf = new("ident_bf", [P, P], BF16)
+        make_identity(nc, ident_bf[:])
+        sign = new("sign", [P, P * L], F32)
+        nc.gpsimd.memset(sign[:], SCORE_SCALE)
+        nc.gpsimd.affine_select(
+            out=sign[:], in_=sign[:], pattern=[[-1, P], [0, L]], compare_op=ALU.not_equal,
+            fill=-SCORE_SCALE, base=0, channel_multiplier=1,
+        )
+
+        x_rows = x_bytes.rearrange("j l k -> (j l) k")
+
+        def load_x(h):
+            raw = new("x_raw%d" % h, [P, L * D], U8)
+            nc.sync.dma_start(out=raw[:], in_=x_rows[HALF * h : HALF * (h + 1), :].rearrange("(p r) k -> p (r k)", r=L))
+            return raw
+
+        def load_w(name, w, g):
+            raw = new("%s_raw%d" % (name, g), [P, PACK, HALF], BF16)
+            nc.sync.dma_start(out=raw[:], in_=w[:, HALF * g : HALF * (g + 1)].rearrange("(p j) c -> p j c", j=PACK))
+            return raw
+
+        x_raw, wu_raw, wg_raw = {}, {}, {}
+        scale4 = new("scale4", [P, PACK], F32)
+        nc.sync.dma_start(out=scale4[:], in_=x_scale.rearrange("a b (p t) -> p (a b t)", t=PACK))
+        wu_raw[0] = load_w("wu", wu, 0)
+        x_raw[0] = load_x(0)
+        wu_raw[1] = load_w("wu", wu, 1)
+        x_raw[1] = load_x(1)
+        for v, vec in enumerate((bu, bg, gain)):
+            nc.sync.dma_start(
+                out=rows[PACK * v : PACK * (v + 1), :].rearrange("t (c r) -> t c r", r=8),
+                in_=vec.rearrange("(c t r) -> t c r", t=PACK, r=8),
+            )
+        y_raw = new("y_raw", [P, 2 * D], BF16)
+        nc.sync.dma_start(out=y_raw[:], in_=y.rearrange("(p r) k -> p (r k)", r=2))
+        wg_raw[0] = load_w("wg", wg, 0)
+        wg_raw[1] = load_w("wg", wg, 1)
+
+        def turn_pair(first, second):
+            bank = turn.tile([P, PACK, P], F32, name="turn_bank")
+            for r, src in enumerate((first, second)):
+                words = src.bitcast(F32)
+                for u in range(2):
+                    nc.tensor.transpose(bank[:, 2 * r + u, :], words[:, u : 2 * P : 2], ident[:])
+            return bank
+
+        def widen_pair(h, a):
+            wide = []
+            for r in (2 * a, 2 * a + 1):
+                row = new("x_wide%d%d" % (h, r), [P, D], BF16)
+                nc.vector.tensor_tensor(
+                    out=row[:], in0=x_raw[h][:, D * r : D * (r + 1)].bitcast(FP8), in1=scale_all[:], op=ALU.mult
+                )
+                wide.append(row)
+            return turn_pair(wide[0][:], wide[1][:])
+
+        x_grouped = [new("x_grouped%d" % h, [P, HALF * PACK], BF16) for h in range(2)]
+
+        def empty_x(h, a, bank):
+            words = x_grouped[h][:].bitcast(F32).rearrange("p (n a q) -> p n a q", a=2, q=PACK)
+            nc.scalar.copy(out=words[:, :, a, :], in_=bank[:].rearrange("p q n -> p n q"))
+
+        def interleave_w(copy, grouped, raw, a):
+            src = raw[:].rearrange("p j (q t r) -> p t q r j", t=PACK, r=8)
+            dst = grouped[:].rearrange("p (t q r j) -> p t q r j", t=PACK, r=8, j=PACK)
+            copy(out=dst[:, 2 * a : 2 * a + 2], in_=src[:, 2 * a : 2 * a + 2])
+
+        wu_grouped = [new("wu_grouped%d" % g, [P, HALF * PACK], BF16) for g in range(2)]
+        wg_grouped = [new("wg_grouped%d" % g, [P, HALF * PACK], BF16) for g in range(2)]
+
+        on_vector, on_scalar = nc.vector.tensor_copy, nc.scalar.copy
+        x_q, wu_q, wg_q, u_q = {}, {}, {}, {}
+
+        def fill_direct(n0, n, g):
+            banks = []
+            for c in range(n // P):
+                acc = mm.tile([P, PACK, P], F32, name="mm_bank")
+                for t in range(PACK):
+                    matmul(acc[:, t, :], wu_q[g], P * t, x_q[n0 // HALF], n0 % HALF + P * c, P)
+                banks.append(acc)
+            return banks
+
+        def empty_direct(grouped, g, banks, first, count):
+            bias = vecs[:, g, 0:PACK].unsqueeze(1).to_broadcast([P, P, PACK])
+            for c in range(first, first + count):
+                nc.vector.tensor_tensor(
+                    out=grouped[:, HALF * c : HALF * (c + 1)].rearrange("p (n t) -> p n t", t=PACK),
+                    in0=banks[c][:].rearrange("p t n -> p n t"), in1=bias, op=ALU.add,
+                )
+
+        def local_planes(pool, tag, n0, n, g):
+            planes = new("u_planes%d_%d" % (n0, g), [P, PACK, n], BF16)
+            per_bank = HALF // n
+            for a in range(PACK // per_bank):
+                acc = pool.tile([P, per_bank, n], F32, name=tag)
+                ts = range(per_bank * a, per_bank * (a + 1))
+                for s, t in enumerate(ts):
+                    matmul(acc[:, s, :], wu_q[g], P * t, x_q[n0 // HALF], n0 % HALF, n)
+                for s, t in enumerate(ts):
+                    nc.scalar.activation(out=planes[:, t, :], in_=acc[:, s, :], func=ACT.Identity, bias=vecs[:, g, t : t + 1])
+            return planes
+
+        def interleave_planes(n0, n, g, planes):
+            grouped = new("u_grouped%d_%d" % (n0, g), [P, n * PACK], BF16)
+            nc.vector.tensor_copy(out=grouped[:].rearrange("p (n t) -> p n t", t=PACK), in_=planes[:].rearrange("p t n -> p n t"))
+            return grouped
+
+        def global_gelu(g):
+            planes = new("g_planes%d" % g, [P, PACK, B], F32)
+            for a in range(2):
+                acc = score.tile([P, 2, B], F32, name="score_bank")
+                for s in range(2):
+                    matmul(acc[:, s, :], wg_q[g], P * (2 * a + s), y_q, 0, B)
+                for s in range(2):
+                    t = 2 * a + s
+                    nc.scalar.activation(
+                        out=planes[:, t, :], in_=acc[:, s, :], func=ACT.Gelu, bias=vecs[:, g, PACK + t : PACK + t + 1]
+                    )
+            return planes
+
+        def global_gain(g, planes):
+            grouped = new("g_grouped%d" % g, [P, B * PACK], BF16)
+            nc.vector.tensor_tensor(
+                out=grouped[:].rearrange("p (n t) -> p n t", t=PACK),
+                in0=planes[:].rearrange("p t n -> p n t"),
+                in1=vecs[:, g, 2 * PACK : 3 * PACK].unsqueeze(1).to_broadcast([P, B, PACK]),
+                op=ALU.mult,
+            )
+            return grouped
+
+        def spread_scale():
+            bank = turn.tile([P, PACK, P], F32, name="turn_bank")
+            for t in range(PACK):
+                nc.tensor.transpose(bank[:, t, :], scale4[:, t : t + 1].to_broadcast([P, P]), ident[:])
+            nc.scalar.copy(out=scale_all[:].rearrange("p (n t) -> p n t", t=PACK), in_=bank[:].rearrange("p t n -> p n t"))
+
+        def turn_vectors():
+            bank = mm.tile([P, 2, P], BF16, name="mm_bank")
+            for g in range(2):
+                nc.tensor.transpose(bank[:, g, :], rows[:, P * g : P * (g + 1)], ident_bf[:])
+            nc.scalar.activation(out=vecs[:], in_=bank[:, :, 0 : 3 * PACK], func=ACT.Copy)
+
+        def turn_y():
+            bank = turn_pair(y_raw[:, 0:D], y_raw[:, D : 2 * D])
+            nc.scalar.copy(
+                out=y_grouped[:].bitcast(F32).rearrange("p (n q) -> p n q", q=PACK), in_=bank[:].rearrange("p q n -> p n q")
+            )
+
+        scale_all = new("scale_all", [P, D], F32)
+        vecs = new("vecs", [P, 2, 3 * PACK], F32)
+        y_grouped = new("y_grouped", [P, B * PACK], BF16)
+        g_q = {}
+        QUARTER = HALF // 2
+        acc_of, signed, capped, exps = {}, {}, {}, {}
+
+        def diagonal(it, n0):
+            return it == n0 // HALF
+
+        def scores(pool, tag, it, n0, n):
+            acc = pool.tile([P, n], F32, name=tag)
+            for g in range(2):
+                matmul(acc[:], g_q[g], P * it, u_q[n0, g], 0, n, start=(g == 0), stop=(g == 1))
+            acc_of[it, n0] = acc
+
+        def flip(it, n0, n):
+            signed[it, n0] = new("signed%d" % n0, [P, n], F32)
+            nc.vector.tensor_tensor(
+                out=signed[it, n0][:], in0=acc_of[it, n0][:], in1=sign[:, n0 % HALF : n0 % HALF + n], op=ALU.mult
+            )
+
+        def exp(it, n0, n):
+            e = new("exp%d_%d" % (it, n0), [P, n], F32)
+            if diagonal(it, n0):
+                nc.scalar.activation(out=e[:], in_=signed[it, n0][:], func=ACT.Exp)
+            else:
+                nc.scalar.activation(out=e[:], in_=acc_of[it, n0][:], func=ACT.Exp, scale=SCORE_SCALE)
+            exps[it, n0] = e
+
+        def cap(it, n0, n):
+            capped[it, n0] = new("capped%d_%d" % (it, n0), [P, n], F32)
+            nc.vector.tensor_scalar(out=capped[it, n0][:], in0=exps[it, n0][:], scalar1=EXP_CAP, scalar2=None, op0=ALU.min)
+
+        spread_scale()
+        interleave_w(on_vector, wu_grouped[0], wu_raw[0], 0)
+        interleave_w(on_scalar, wu_grouped[0], wu_raw[0], 1)
+        b00 = widen_pair(0, 0)
+        b01 = widen_pair(0, 1)
+        interleave_w(on_scalar, wu_grouped[1], wu_raw[1], 0)
+        wu_q[0] = quantize("wu0", wu_grouped[0])
+        empty_x(0, 0, b00)
+        empty_x(0, 1, b01)
+        turn_vectors()
+        b10 = widen_pair(1, 0)
+        interleave_w(on_scalar, wu_grouped[1], wu_raw[1], 1)
+        x_q[0] = quantize("x0", x_grouped[0])
+        empty_x(1, 0, b10)
+        turn_y()
+        fa0 = fill_direct(0, HALF, 0)
+        b11 = widen_pair(1, 1)
+        interleave_w(on_scalar, wg_grouped[0], wg_raw[0], 0)
+        empty_x(1, 1, b11)
+        interleave_w(on_scalar, wg_grouped[0], wg_raw[0], 1)
+        ua0 = new("ua0_grouped", [P, HALF * PACK], BF16)
+        empty_direct(ua0, 0, fa0, 0, 4)
+        wu_q[1] = quantize("wu1", wu_grouped[1])
+        fa1 = fill_direct(0, HALF, 1)
+        u_q[0, 0] = quantize("ua0", ua0)
+        y_q = quantize("y", y_grouped)
+        x_q[1] = quantize("x1", x_grouped[1])
+        wg_q[0] = quantize("wg0", wg_grouped[0])
+        interleave_w(on_scalar, wg_grouped[1], wg_raw[1], 0)
+        interleave_w(on_scalar, wg_grouped[1], wg_raw[1], 1)
+        gp0 = global_gelu(0)
+        ua1 = new("ua1_grouped", [P, HALF * PACK], BF16)
+        empty_direct(ua1, 1, fa1, 0, 2)
+        wg_q[1] = quantize("wg1", wg_grouped[1])
+        empty_direct(ua1, 1, fa1, 2, 2)
+        gp1 = global_gelu(1)
+        u_q[0, 1] = quantize("ua1", ua1)
+        ph0 = local_planes(mm, "mm_bank", HALF, HALF, 0)
+        gg0 = global_gain(0, gp0)
+        gg1 = global_gain(1, gp1)
+        pb1 = local_planes(turn, "turn_bank", HALF, QUARTER, 1)
+        pc1 = local_planes(mm, "mm_bank", HALF + QUARTER, QUARTER, 1)
+        g_q[0] = quantize("g0", gg0)
+        g_q[1] = quantize("g1", gg1)
+        scores(score, "score_bank", 0, 0, HALF)
+        scores(score, "score_bank", 1, 0, HALF)
+        uh0 = interleave_planes(HALF, HALF, 0, ph0)
+        flip(0, 0, HALF)
+        u_h1 = quantize("uh0", uh0)
+        u_q[HALF, 0] = (u_h1[0][:, 0:QUARTER], u_h1[1][:, 0:QUARTER])
+        u_q[HALF + QUARTER, 0] = (u_h1[0][:, QUARTER:HALF], u_h1[1][:, QUARTER:HALF])
+        ub1 = interleave_planes(HALF, QUARTER, 1, pb1)
+        uc1 = interleave_planes(HALF + QUARTER, QUARTER, 1, pc1)
+        u_q[HALF, 1] = quantize("ub1", ub1)
+        u_q[HALF + QUARTER, 1] = quantize("uc1", uc1)
+        scores(turn, "turn_bank", 1, HALF, QUARTER)
+        scores(turn, "turn_bank", 0, HALF, QUARTER)
+        scores(mm, "mm_bank", 1, HALF + QUARTER, QUARTER)
+        scores(mm, "mm_bank", 0, HALF + QUARTER, QUARTER)
+        flip(1, HALF, QUARTER)
+        flip(1, HALF + QUARTER, QUARTER)
+        blocks = [(1, 0, HALF), (0, 0, HALF), (0, HALF, QUARTER), (1, HALF, QUARTER), (0, HALF + QUARTER, QUARTER), (1, HALF + QUARTER, QUARTER)]
+        for blk in blocks:
+            exp(*blk)
+        for blk in blocks:
+            cap(*blk)
+        out_rows = out.rearrange("i j l -> i (j l)")
+        for it, n0, n in blocks:
+            ln = new("ln%d_%d" % (it, n0), [P, n], F32)
+            nc.scalar.activation(out=ln[:], in_=capped[it, n0][:], func=ACT.Ln, bias=1.0)
+            res = new("res%d_%d" % (it, n0), [P, n], F32)
+            if diagonal(it, n0):
+                nc.vector.tensor_tensor(out=res[:], in0=signed[it, n0][:], in1=ln[:], op=ALU.max)
+            else:
+                nc.vector.scalar_tensor_tensor(
+                    out=res[:], in0=acc_of[it, n0][:], scalar=SCORE_SCALE, in1=ln[:], op0=ALU.mult, op1=ALU.max
+                )
+            nc.sync.dma_start(out=out_rows[P * it : P * (it + 1), n0 : n0 + n], in_=res[:])

@@ -52,17 +52,15 @@ def tile_deepinfomaxlocalglobaljsdmap_kernel(tc, x_bytes, x_scale, y, wu, bu, wg
                 stop=stop,
             )
 
-        rows = new("rows", [P, 2 * P], BF16)
-        nc.vector.memset(rows[:], 0.0)
+        warm = new("warm", [P, 2], F32)
+        nc.vector.memset(warm[:, 0:1], 0.0)
+        nc.scalar.activation(out=warm[:, 1:2], in_=warm[:, 0:1], func=ACT.Gelu)
         ident = new("ident", [P, P], F32)
         make_identity(nc, ident[:])
-        ident_bf = new("ident_bf", [P, P], BF16)
-        make_identity(nc, ident_bf[:])
         sign = new("sign", [P, P * L], F32)
-        nc.gpsimd.memset(sign[:], SCORE_SCALE)
-        nc.gpsimd.affine_select(
-            out=sign[:], in_=sign[:], pattern=[[-1, P], [0, L]], compare_op=ALU.not_equal,
-            fill=-SCORE_SCALE, base=0, channel_multiplier=1,
+        nc.vector.tensor_scalar(
+            out=sign[:].rearrange("p (j l) -> p j l", l=L), in0=ident[:].unsqueeze(2).to_broadcast([P, P, L]),
+            scalar1=-2.0 * SCORE_SCALE, scalar2=SCORE_SCALE, op0=ALU.mult, op1=ALU.add,
         )
 
         x_rows = x_bytes.rearrange("j l k -> (j l) k")
@@ -82,20 +80,20 @@ def tile_deepinfomaxlocalglobaljsdmap_kernel(tc, x_bytes, x_scale, y, wu, bu, wg
         nc.sync.dma_start(out=scale4[:], in_=x_scale.rearrange("a b (p t) -> p (a b t)", t=PACK))
         wu_raw[0] = load_w("wu", wu, 0)
         x_raw[0] = load_x(0)
-        wu_raw[1] = load_w("wu", wu, 1)
-        x_raw[1] = load_x(1)
-        for v, vec in enumerate((bu, bg, gain)):
-            nc.sync.dma_start(
-                out=rows[PACK * v : PACK * (v + 1), :].rearrange("t (c r) -> t c r", r=8),
-                in_=vec.rearrange("(c t r) -> t c r", t=PACK, r=8),
-            )
+        wg_raw[0] = load_w("wg", wg, 0)
         y_raw = new("y_raw", [P, 2 * D], BF16)
         nc.sync.dma_start(out=y_raw[:], in_=y.rearrange("(p r) k -> p (r k)", r=2))
-        wg_raw[0] = load_w("wg", wg, 0)
+        vec_raw = []
+        for name, vec in (("bu", bu), ("bg", bg), ("gain", gain)):
+            raw = new(name + "_raw", [P, 2, PACK], BF16)
+            nc.sync.dma_start(out=raw[:], in_=vec.rearrange("(g p t) -> p g t", g=2, t=PACK))
+            vec_raw.append(raw)
+        x_raw[1] = load_x(1)
+        wu_raw[1] = load_w("wu", wu, 1)
         wg_raw[1] = load_w("wg", wg, 1)
 
-        def turn_pair(first, second):
-            bank = turn.tile([P, PACK, P], F32, name="turn_bank")
+        def turn_pair(pool, tag, first, second):
+            bank = pool.tile([P, PACK, P], F32, name=tag)
             for r, src in enumerate((first, second)):
                 words = src.bitcast(F32)
                 for u in range(2):
@@ -110,7 +108,7 @@ def tile_deepinfomaxlocalglobaljsdmap_kernel(tc, x_bytes, x_scale, y, wu, bu, wg
                     out=row[:], in0=x_raw[h][:, D * r : D * (r + 1)].bitcast(FP8), in1=scale_all[:], op=ALU.mult
                 )
                 wide.append(row)
-            return turn_pair(wide[0][:], wide[1][:])
+            return turn_pair(turn, "turn_bank", wide[0][:], wide[1][:])
 
         x_grouped = [new("x_grouped%d" % h, [P, HALF * PACK], BF16) for h in range(2)]
 
@@ -119,9 +117,10 @@ def tile_deepinfomaxlocalglobaljsdmap_kernel(tc, x_bytes, x_scale, y, wu, bu, wg
             nc.scalar.copy(out=words[:, :, a, :], in_=bank[:].rearrange("p q n -> p n q"))
 
         def interleave_w(copy, grouped, raw, a):
-            src = raw[:].rearrange("p j (q t r) -> p t q r j", t=PACK, r=8)
-            dst = grouped[:].rearrange("p (t q r j) -> p t q r j", t=PACK, r=8, j=PACK)
-            copy(out=dst[:, 2 * a : 2 * a + 2], in_=src[:, 2 * a : 2 * a + 2])
+            src = raw[:].rearrange("p j (m t) -> p m j t", t=PACK)
+            dst = grouped[:].rearrange("p (t m j) -> p m j t", t=PACK, j=PACK)
+            half = slice(P // 2 * a, P // 2 * (a + 1))
+            copy(out=dst[:, half], in_=src[:, half])
 
         wu_grouped = [new("wu_grouped%d" % g, [P, HALF * PACK], BF16) for g in range(2)]
         wg_grouped = [new("wg_grouped%d" % g, [P, HALF * PACK], BF16) for g in range(2)]
@@ -158,9 +157,15 @@ def tile_deepinfomaxlocalglobaljsdmap_kernel(tc, x_bytes, x_scale, y, wu, bu, wg
                     nc.scalar.activation(out=planes[:, t, :], in_=acc[:, s, :], func=ACT.Identity, bias=vecs[:, g, t : t + 1])
             return planes
 
+        def interleave(grouped, planes):
+            nc.vector.tensor_copy(
+                out=grouped[:].rearrange("p (c i t) -> p c t i", i=PACK, t=PACK),
+                in_=planes[:].rearrange("p t (c i) -> p c t i", i=PACK),
+            )
+
         def interleave_planes(n0, n, g, planes):
             grouped = new("u_grouped%d_%d" % (n0, g), [P, n * PACK], BF16)
-            nc.vector.tensor_copy(out=grouped[:].rearrange("p (n t) -> p n t", t=PACK), in_=planes[:].rearrange("p t n -> p n t"))
+            interleave(grouped, planes)
             return grouped
 
         def global_gelu(g):
@@ -177,13 +182,17 @@ def tile_deepinfomaxlocalglobaljsdmap_kernel(tc, x_bytes, x_scale, y, wu, bu, wg
             return planes
 
         def global_gain(g, planes):
+            gained = new("g_gained%d" % g, [P, PACK, B], BF16)
+            for t in range(PACK):
+                nc.vector.tensor_scalar(
+                    out=gained[:, t, :], in0=planes[:, t, :], scalar1=vecs[:, g, 2 * PACK + t : 2 * PACK + t + 1],
+                    scalar2=None, op0=ALU.mult,
+                )
+            return gained
+
+        def interleave_global(g, gained):
             grouped = new("g_grouped%d" % g, [P, B * PACK], BF16)
-            nc.vector.tensor_tensor(
-                out=grouped[:].rearrange("p (n t) -> p n t", t=PACK),
-                in0=planes[:].rearrange("p t n -> p n t"),
-                in1=vecs[:, g, 2 * PACK : 3 * PACK].unsqueeze(1).to_broadcast([P, B, PACK]),
-                op=ALU.mult,
-            )
+            interleave(grouped, gained)
             return grouped
 
         def spread_scale():
@@ -192,14 +201,11 @@ def tile_deepinfomaxlocalglobaljsdmap_kernel(tc, x_bytes, x_scale, y, wu, bu, wg
                 nc.tensor.transpose(bank[:, t, :], scale4[:, t : t + 1].to_broadcast([P, P]), ident[:])
             nc.scalar.copy(out=scale_all[:].rearrange("p (n t) -> p n t", t=PACK), in_=bank[:].rearrange("p t n -> p n t"))
 
-        def turn_vectors():
-            bank = mm.tile([P, 2, P], BF16, name="mm_bank")
-            for g in range(2):
-                nc.tensor.transpose(bank[:, g, :], rows[:, P * g : P * (g + 1)], ident_bf[:])
-            nc.scalar.activation(out=vecs[:], in_=bank[:, :, 0 : 3 * PACK], func=ACT.Copy)
+        def widen_vectors():
+            for v in range(3):
+                nc.scalar.copy(out=vecs[:, :, PACK * v : PACK * (v + 1)], in_=vec_raw[v][:])
 
-        def turn_y():
-            bank = turn_pair(y_raw[:, 0:D], y_raw[:, D : 2 * D])
+        def empty_y(bank):
             nc.scalar.copy(
                 out=y_grouped[:].bitcast(F32).rearrange("p (n q) -> p n q", q=PACK), in_=bank[:].rearrange("p q n -> p n q")
             )
@@ -242,64 +248,64 @@ def tile_deepinfomaxlocalglobaljsdmap_kernel(tc, x_bytes, x_scale, y, wu, bu, wg
         interleave_w(on_vector, wu_grouped[0], wu_raw[0], 0)
         interleave_w(on_scalar, wu_grouped[0], wu_raw[0], 1)
         b00 = widen_pair(0, 0)
+        interleave_w(on_scalar, wg_grouped[0], wg_raw[0], 0)
         b01 = widen_pair(0, 1)
-        interleave_w(on_scalar, wu_grouped[1], wu_raw[1], 0)
+        by = turn_pair(mm, "mm_bank", y_raw[:, 0:D], y_raw[:, D : 2 * D])
         wu_q[0] = quantize("wu0", wu_grouped[0])
         empty_x(0, 0, b00)
         empty_x(0, 1, b01)
-        turn_vectors()
         b10 = widen_pair(1, 0)
-        interleave_w(on_scalar, wu_grouped[1], wu_raw[1], 1)
         x_q[0] = quantize("x0", x_grouped[0])
-        empty_x(1, 0, b10)
-        turn_y()
-        fa0 = fill_direct(0, HALF, 0)
-        b11 = widen_pair(1, 1)
-        interleave_w(on_scalar, wg_grouped[0], wg_raw[0], 0)
-        empty_x(1, 1, b11)
+        empty_y(by)
+        widen_vectors()
         interleave_w(on_scalar, wg_grouped[0], wg_raw[0], 1)
-        ua0 = new("ua0_grouped", [P, HALF * PACK], BF16)
-        empty_direct(ua0, 0, fa0, 0, 4)
-        wu_q[1] = quantize("wu1", wu_grouped[1])
-        fa1 = fill_direct(0, HALF, 1)
-        u_q[0, 0] = quantize("ua0", ua0)
+        empty_x(1, 0, b10)
+        pa0 = local_planes(mm, "mm_bank", 0, HALF, 0)
+        b11 = widen_pair(1, 1)
+        empty_x(1, 1, b11)
         y_q = quantize("y", y_grouped)
-        x_q[1] = quantize("x1", x_grouped[1])
+        interleave_w(on_vector, wu_grouped[1], wu_raw[1], 0)
+        interleave_w(on_vector, wu_grouped[1], wu_raw[1], 1)
         wg_q[0] = quantize("wg0", wg_grouped[0])
-        interleave_w(on_scalar, wg_grouped[1], wg_raw[1], 0)
-        interleave_w(on_scalar, wg_grouped[1], wg_raw[1], 1)
         gp0 = global_gelu(0)
-        ua1 = new("ua1_grouped", [P, HALF * PACK], BF16)
-        empty_direct(ua1, 1, fa1, 0, 2)
-        wg_q[1] = quantize("wg1", wg_grouped[1])
-        empty_direct(ua1, 1, fa1, 2, 2)
-        gp1 = global_gelu(1)
-        u_q[0, 1] = quantize("ua1", ua1)
-        ph0 = local_planes(mm, "mm_bank", HALF, HALF, 0)
+        wu_q[1] = quantize("wu1", wu_grouped[1])
+        ua0 = interleave_planes(0, HALF, 0, pa0)
+        interleave_w(on_vector, wg_grouped[1], wg_raw[1], 0)
+        interleave_w(on_scalar, wg_grouped[1], wg_raw[1], 1)
+        pa1 = local_planes(mm, "mm_bank", 0, HALF, 1)
+        x_q[1] = quantize("x1", x_grouped[1])
+        u_q[0, 0] = quantize("ua0", ua0)
         gg0 = global_gain(0, gp0)
+        wg_q[1] = quantize("wg1", wg_grouped[1])
+        gp1 = global_gelu(1)
+        gi0 = interleave_global(0, gg0)
+        ua1 = interleave_planes(0, HALF, 1, pa1)
+        g_q[0] = quantize("g0", gi0)
+        ph0 = local_planes(mm, "mm_bank", HALF, HALF, 0)
         gg1 = global_gain(1, gp1)
+        u_q[0, 1] = quantize("ua1", ua1)
+        gi1 = interleave_global(1, gg1)
         pb1 = local_planes(turn, "turn_bank", HALF, QUARTER, 1)
         pc1 = local_planes(mm, "mm_bank", HALF + QUARTER, QUARTER, 1)
-        g_q[0] = quantize("g0", gg0)
-        g_q[1] = quantize("g1", gg1)
+        uh0 = interleave_planes(HALF, HALF, 0, ph0)
+        g_q[1] = quantize("g1", gi1)
         scores(score, "score_bank", 0, 0, HALF)
         scores(score, "score_bank", 1, 0, HALF)
-        uh0 = interleave_planes(HALF, HALF, 0, ph0)
-        flip(0, 0, HALF)
+        ub1 = interleave_planes(HALF, QUARTER, 1, pb1)
         u_h1 = quantize("uh0", uh0)
         u_q[HALF, 0] = (u_h1[0][:, 0:QUARTER], u_h1[1][:, 0:QUARTER])
         u_q[HALF + QUARTER, 0] = (u_h1[0][:, QUARTER:HALF], u_h1[1][:, QUARTER:HALF])
-        ub1 = interleave_planes(HALF, QUARTER, 1, pb1)
-        uc1 = interleave_planes(HALF + QUARTER, QUARTER, 1, pc1)
         u_q[HALF, 1] = quantize("ub1", ub1)
-        u_q[HALF + QUARTER, 1] = quantize("uc1", uc1)
+        uc1 = interleave_planes(HALF + QUARTER, QUARTER, 1, pc1)
         scores(turn, "turn_bank", 1, HALF, QUARTER)
         scores(turn, "turn_bank", 0, HALF, QUARTER)
+        flip(0, 0, HALF)
+        u_q[HALF + QUARTER, 1] = quantize("uc1", uc1)
         scores(mm, "mm_bank", 1, HALF + QUARTER, QUARTER)
         scores(mm, "mm_bank", 0, HALF + QUARTER, QUARTER)
         flip(1, HALF, QUARTER)
         flip(1, HALF + QUARTER, QUARTER)
-        blocks = [(1, 0, HALF), (0, 0, HALF), (0, HALF, QUARTER), (1, HALF, QUARTER), (0, HALF + QUARTER, QUARTER), (1, HALF + QUARTER, QUARTER)]
+        blocks = [(1, 0, HALF), (0, HALF, QUARTER), (0, 0, HALF), (1, HALF, QUARTER), (0, HALF + QUARTER, QUARTER), (1, HALF + QUARTER, QUARTER)]
         for blk in blocks:
             exp(*blk)
         for blk in blocks:

@@ -18,6 +18,7 @@ ACT = mybir.ActivationFunctionType
 P = 128
 PACK = 4
 HALF = 512
+QUARTER = 256
 SCORE_SCALE = 1.0 / 16.0
 EXP_CAP = 2.0 ** 60
 
@@ -70,27 +71,42 @@ def tile_deepinfomaxlocalglobaljsdmap_kernel(tc, x_bytes, x_scale, y, wu, bu, wg
             nc.sync.dma_start(out=raw[:], in_=x_rows[HALF * h : HALF * (h + 1), :].rearrange("(p r) k -> p (r k)", r=L))
             return raw
 
-        def load_w(name, w, g):
-            raw = new("%s_raw%d" % (name, g), [P, PACK, HALF], BF16)
-            nc.sync.dma_start(out=raw[:], in_=w[:, HALF * g : HALF * (g + 1)].rearrange("(p j) c -> p j c", j=PACK))
-            return raw
+        def load_w(name, w, g, a, halves):
+            width = QUARTER * halves
+            c0 = HALF * g + QUARTER * a
+            raw = new("%s_raw%d%d" % (name, g, a), [P, PACK, width], BF16)
+            nc.sync.dma_start(out=raw[:], in_=w[:, c0 : c0 + width].rearrange("(p j) c -> p j c", j=PACK))
+            for b in range(halves):
+                w_raw[name, g, a + b] = raw[:, :, QUARTER * b : QUARTER * (b + 1)]
 
         x_raw, wu_raw, wg_raw = {}, {}, {}
+        w_raw = {}
         scale4 = new("scale4", [P, PACK], F32)
         nc.sync.dma_start(out=scale4[:], in_=x_scale.rearrange("a b (p t) -> p (a b t)", t=PACK))
-        wu_raw[0] = load_w("wu", wu, 0)
+        load_w("wu", wu, 0, 0, 1)
+        load_w("wu", wu, 0, 1, 1)
         x_raw[0] = load_x(0)
-        wg_raw[0] = load_w("wg", wg, 0)
+        load_w("wg", wg, 0, 0, 1)
+        load_w("wg", wg, 0, 1, 1)
         y_raw = new("y_raw", [P, 2 * D], BF16)
         nc.sync.dma_start(out=y_raw[:], in_=y.rearrange("(p r) k -> p (r k)", r=2))
+        x_raw[1] = load_x(1)
         vec_raw = []
         for name, vec in (("bu", bu), ("bg", bg), ("gain", gain)):
             raw = new(name + "_raw", [P, 2, PACK], BF16)
             nc.sync.dma_start(out=raw[:], in_=vec.rearrange("(g p t) -> p g t", g=2, t=PACK))
             vec_raw.append(raw)
-        x_raw[1] = load_x(1)
-        wu_raw[1] = load_w("wu", wu, 1)
-        wg_raw[1] = load_w("wg", wg, 1)
+        load_w("wu", wu, 1, 0, 2)
+        load_w("wg", wg, 1, 0, 2)
+
+        def by_pairs(planes):
+            return planes[:].rearrange("p t (c i) -> p c t i", i=2)
+
+        def into_pairs(flat):
+            return flat.rearrange("p (c i t) -> p c t i", i=2, t=PACK)
+
+        def per_plane(values, n):
+            return values.unsqueeze(1).unsqueeze(3).to_broadcast([P, n // 2, PACK, 2])
 
         def turn_pair(pool, tag, first, second):
             bank = pool.tile([P, PACK, P], F32, name=tag)
@@ -113,37 +129,36 @@ def tile_deepinfomaxlocalglobaljsdmap_kernel(tc, x_bytes, x_scale, y, wu, bu, wg
         x_grouped = [new("x_grouped%d" % h, [P, HALF * PACK], BF16) for h in range(2)]
 
         def empty_x(h, a, bank):
-            words = x_grouped[h][:].bitcast(F32).rearrange("p (n a q) -> p n a q", a=2, q=PACK)
-            nc.scalar.copy(out=words[:, :, a, :], in_=bank[:].rearrange("p q n -> p n q"))
+            words = x_grouped[h][:].bitcast(F32).rearrange("p (c i a q) -> p a c q i", i=2, a=2, q=PACK)
+            nc.scalar.copy(out=words[:, a], in_=by_pairs(bank))
 
-        def interleave_w(copy, grouped, raw, a):
-            src = raw[:].rearrange("p j (m t) -> p m j t", t=PACK)
-            dst = grouped[:].rearrange("p (t m j) -> p m j t", t=PACK, j=PACK)
-            half = slice(P // 2 * a, P // 2 * (a + 1))
-            copy(out=dst[:, half], in_=src[:, half])
+        def interleave_w(copy, name, g, a):
+            src = w_raw[name, g, a].rearrange("p j (m t) -> p m j t", t=PACK)
+            dst = w_grouped[name, g][:].rearrange("p (t m j) -> p m j t", t=PACK, j=PACK)
+            copy(out=dst[:, P // 2 * a : P // 2 * (a + 1)], in_=src)
 
-        wu_grouped = [new("wu_grouped%d" % g, [P, HALF * PACK], BF16) for g in range(2)]
-        wg_grouped = [new("wg_grouped%d" % g, [P, HALF * PACK], BF16) for g in range(2)]
+        w_grouped = {(name, g): new("%s_grouped%d" % (name, g), [P, HALF * PACK], BF16) for name in ("wu", "wg") for g in range(2)}
 
         on_vector, on_scalar = nc.vector.tensor_copy, nc.scalar.copy
         x_q, wu_q, wg_q, u_q = {}, {}, {}, {}
 
-        def fill_direct(n0, n, g):
+        def fill_direct(pool, tag, n0, n, g):
             banks = []
             for c in range(n // P):
-                acc = mm.tile([P, PACK, P], F32, name="mm_bank")
+                acc = pool.tile([P, PACK, P], F32, name=tag)
                 for t in range(PACK):
                     matmul(acc[:, t, :], wu_q[g], P * t, x_q[n0 // HALF], n0 % HALF + P * c, P)
                 banks.append(acc)
             return banks
 
-        def empty_direct(grouped, g, banks, first, count):
-            bias = vecs[:, g, 0:PACK].unsqueeze(1).to_broadcast([P, P, PACK])
-            for c in range(first, first + count):
+        def empty_direct(n0, n, g, banks):
+            grouped = new("u_grouped%d_%d" % (n0, g), [P, n * PACK], BF16)
+            for c, acc in enumerate(banks):
                 nc.vector.tensor_tensor(
-                    out=grouped[:, HALF * c : HALF * (c + 1)].rearrange("p (n t) -> p n t", t=PACK),
-                    in0=banks[c][:].rearrange("p t n -> p n t"), in1=bias, op=ALU.add,
+                    out=into_pairs(grouped[:, HALF * c : HALF * (c + 1)]), in0=by_pairs(acc),
+                    in1=per_plane(vecs[:, g, 0:PACK], P), op=ALU.add,
                 )
+            return grouped
 
         def local_planes(pool, tag, n0, n, g):
             planes = new("u_planes%d_%d" % (n0, g), [P, PACK, n], BF16)
@@ -182,49 +197,36 @@ def tile_deepinfomaxlocalglobaljsdmap_kernel(tc, x_bytes, x_scale, y, wu, bu, wg
             return planes
 
         def global_gain(g, planes):
-            gained = new("g_gained%d" % g, [P, PACK, B], BF16)
-            for t in range(PACK):
-                nc.vector.tensor_scalar(
-                    out=gained[:, t, :], in0=planes[:, t, :], scalar1=vecs[:, g, 2 * PACK + t : 2 * PACK + t + 1],
-                    scalar2=None, op0=ALU.mult,
-                )
-            return gained
-
-        def interleave_global(g, gained):
             grouped = new("g_grouped%d" % g, [P, B * PACK], BF16)
-            interleave(grouped, gained)
+            nc.vector.tensor_tensor(
+                out=into_pairs(grouped[:]), in0=by_pairs(planes), in1=per_plane(vecs[:, g, 2 * PACK : 3 * PACK], B), op=ALU.mult
+            )
             return grouped
 
         def spread_scale():
             bank = turn.tile([P, PACK, P], F32, name="turn_bank")
             for t in range(PACK):
                 nc.tensor.transpose(bank[:, t, :], scale4[:, t : t + 1].to_broadcast([P, P]), ident[:])
-            nc.scalar.copy(out=scale_all[:].rearrange("p (n t) -> p n t", t=PACK), in_=bank[:].rearrange("p t n -> p n t"))
+            nc.scalar.copy(out=into_pairs(scale_all[:]), in_=by_pairs(bank))
 
         def widen_vectors():
             for v in range(3):
                 nc.scalar.copy(out=vecs[:, :, PACK * v : PACK * (v + 1)], in_=vec_raw[v][:])
 
         def empty_y(bank):
-            nc.scalar.copy(
-                out=y_grouped[:].bitcast(F32).rearrange("p (n q) -> p n q", q=PACK), in_=bank[:].rearrange("p q n -> p n q")
-            )
+            nc.scalar.copy(out=into_pairs(y_grouped[:].bitcast(F32)), in_=by_pairs(bank))
 
         scale_all = new("scale_all", [P, D], F32)
         vecs = new("vecs", [P, 2, 3 * PACK], F32)
         y_grouped = new("y_grouped", [P, B * PACK], BF16)
         g_q = {}
-        QUARTER = HALF // 2
         acc_of, signed, capped, exps = {}, {}, {}, {}
 
         def diagonal(it, n0):
             return it == n0 // HALF
 
-        def scores(pool, tag, it, n0, n):
-            acc = pool.tile([P, n], F32, name=tag)
-            for g in range(2):
-                matmul(acc[:], g_q[g], P * it, u_q[n0, g], 0, n, start=(g == 0), stop=(g == 1))
-            acc_of[it, n0] = acc
+        def scores(it, n0, n, g):
+            matmul(acc_of[it, n0][:], g_q[g], P * it, u_q[n0, g], 0, n, start=(g == 0), stop=(g == 1))
 
         def flip(it, n0, n):
             signed[it, n0] = new("signed%d" % n0, [P, n], F32)
@@ -245,80 +247,85 @@ def tile_deepinfomaxlocalglobaljsdmap_kernel(tc, x_bytes, x_scale, y, wu, bu, wg
             nc.vector.tensor_scalar(out=capped[it, n0][:], in0=exps[it, n0][:], scalar1=EXP_CAP, scalar2=None, op0=ALU.min)
 
         spread_scale()
-        interleave_w(on_vector, wu_grouped[0], wu_raw[0], 0)
-        interleave_w(on_scalar, wu_grouped[0], wu_raw[0], 1)
+        interleave_w(on_vector, "wu", 0, 0)
+        interleave_w(on_vector, "wu", 0, 1)
+        interleave_w(on_scalar, "wg", 0, 0)
         b00 = widen_pair(0, 0)
-        interleave_w(on_scalar, wg_grouped[0], wg_raw[0], 0)
+        interleave_w(on_scalar, "wg", 0, 1)
         b01 = widen_pair(0, 1)
         by = turn_pair(mm, "mm_bank", y_raw[:, 0:D], y_raw[:, D : 2 * D])
-        wu_q[0] = quantize("wu0", wu_grouped[0])
+        wu_q[0] = quantize("wu0", w_grouped["wu", 0])
         empty_x(0, 0, b00)
         empty_x(0, 1, b01)
         b10 = widen_pair(1, 0)
         x_q[0] = quantize("x0", x_grouped[0])
         empty_y(by)
         widen_vectors()
-        interleave_w(on_scalar, wg_grouped[0], wg_raw[0], 1)
         empty_x(1, 0, b10)
+        interleave_w(on_scalar, "wu", 1, 0)
         pa0 = local_planes(mm, "mm_bank", 0, HALF, 0)
         b11 = widen_pair(1, 1)
-        empty_x(1, 1, b11)
+        wg_q[0] = quantize("wg0", w_grouped["wg", 0])
         y_q = quantize("y", y_grouped)
-        interleave_w(on_vector, wu_grouped[1], wu_raw[1], 0)
-        interleave_w(on_vector, wu_grouped[1], wu_raw[1], 1)
-        wg_q[0] = quantize("wg0", wg_grouped[0])
+        empty_x(1, 1, b11)
         gp0 = global_gelu(0)
-        wu_q[1] = quantize("wu1", wu_grouped[1])
+        interleave_w(on_vector, "wu", 1, 1)
+        interleave_w(on_vector, "wg", 1, 0)
+        wu_q[1] = quantize("wu1", w_grouped["wu", 1])
+        interleave_w(on_vector, "wg", 1, 1)
         ua0 = interleave_planes(0, HALF, 0, pa0)
-        interleave_w(on_vector, wg_grouped[1], wg_raw[1], 0)
-        interleave_w(on_scalar, wg_grouped[1], wg_raw[1], 1)
         pa1 = local_planes(mm, "mm_bank", 0, HALF, 1)
         x_q[1] = quantize("x1", x_grouped[1])
-        u_q[0, 0] = quantize("ua0", ua0)
-        gg0 = global_gain(0, gp0)
-        wg_q[1] = quantize("wg1", wg_grouped[1])
+        wg_q[1] = quantize("wg1", w_grouped["wg", 1])
         gp1 = global_gelu(1)
-        gi0 = interleave_global(0, gg0)
+        gg0 = global_gain(0, gp0)
+        u_q[0, 0] = quantize("ua0", ua0)
         ua1 = interleave_planes(0, HALF, 1, pa1)
-        g_q[0] = quantize("g0", gi0)
+        g_q[0] = quantize("g0", gg0)
         ph0 = local_planes(mm, "mm_bank", HALF, HALF, 0)
         gg1 = global_gain(1, gp1)
         u_q[0, 1] = quantize("ua1", ua1)
-        gi1 = interleave_global(1, gg1)
+        g_q[1] = quantize("g1", gg1)
         pb1 = local_planes(turn, "turn_bank", HALF, QUARTER, 1)
         pc1 = local_planes(mm, "mm_bank", HALF + QUARTER, QUARTER, 1)
+        for it in (0, 1):
+            acc_of[it, 0] = score.tile([P, HALF], F32, name="score_bank")
+            scores(it, 0, HALF, 0)
+            scores(it, 0, HALF, 1)
         uh0 = interleave_planes(HALF, HALF, 0, ph0)
-        g_q[1] = quantize("g1", gi1)
-        scores(score, "score_bank", 0, 0, HALF)
-        scores(score, "score_bank", 1, 0, HALF)
-        ub1 = interleave_planes(HALF, QUARTER, 1, pb1)
+        flip(0, 0, HALF)
         u_h1 = quantize("uh0", uh0)
         u_q[HALF, 0] = (u_h1[0][:, 0:QUARTER], u_h1[1][:, 0:QUARTER])
         u_q[HALF + QUARTER, 0] = (u_h1[0][:, QUARTER:HALF], u_h1[1][:, QUARTER:HALF])
-        u_q[HALF, 1] = quantize("ub1", ub1)
+        for pool, tag, n0 in ((turn, "turn_bank", HALF), (mm, "mm_bank", HALF + QUARTER)):
+            for it in (1, 0):
+                acc_of[it, n0] = pool.tile([P, QUARTER], F32, name=tag)
+                scores(it, n0, QUARTER, 0)
+        ub1 = interleave_planes(HALF, QUARTER, 1, pb1)
         uc1 = interleave_planes(HALF + QUARTER, QUARTER, 1, pc1)
-        scores(turn, "turn_bank", 1, HALF, QUARTER)
-        scores(turn, "turn_bank", 0, HALF, QUARTER)
-        flip(0, 0, HALF)
+        u_q[HALF, 1] = quantize("ub1", ub1)
         u_q[HALF + QUARTER, 1] = quantize("uc1", uc1)
-        scores(mm, "mm_bank", 1, HALF + QUARTER, QUARTER)
-        scores(mm, "mm_bank", 0, HALF + QUARTER, QUARTER)
+        for n0 in (HALF, HALF + QUARTER):
+            for it in (1, 0):
+                scores(it, n0, QUARTER, 1)
         flip(1, HALF, QUARTER)
         flip(1, HALF + QUARTER, QUARTER)
-        blocks = [(1, 0, HALF), (0, HALF, QUARTER), (0, 0, HALF), (1, HALF, QUARTER), (0, HALF + QUARTER, QUARTER), (1, HALF + QUARTER, QUARTER)]
+        blocks = [(1, 0, HALF), (0, 0, HALF), (0, HALF, QUARTER), (1, HALF, QUARTER), (0, HALF + QUARTER, QUARTER), (1, HALF + QUARTER, QUARTER)]
         for blk in blocks:
             exp(*blk)
         for blk in blocks:
             cap(*blk)
         out_rows = out.rearrange("i j l -> i (j l)")
         for it, n0, n in blocks:
-            ln = new("ln%d_%d" % (it, n0), [P, n], F32)
-            nc.scalar.activation(out=ln[:], in_=capped[it, n0][:], func=ACT.Ln, bias=1.0)
-            res = new("res%d_%d" % (it, n0), [P, n], F32)
-            if diagonal(it, n0):
-                nc.vector.tensor_tensor(out=res[:], in0=signed[it, n0][:], in1=ln[:], op=ALU.max)
-            else:
-                nc.vector.scalar_tensor_tensor(
-                    out=res[:], in0=acc_of[it, n0][:], scalar=SCORE_SCALE, in1=ln[:], op0=ALU.mult, op1=ALU.max
-                )
-            nc.sync.dma_start(out=out_rows[P * it : P * (it + 1), n0 : n0 + n], in_=res[:])
+            for c0 in range(0, n, QUARTER):
+                cols = slice(c0, c0 + QUARTER)
+                ln = new("ln%d_%d" % (it, n0 + c0), [P, QUARTER], F32)
+                nc.scalar.activation(out=ln[:], in_=capped[it, n0][:, cols], func=ACT.Ln, bias=1.0)
+                res = new("res%d_%d" % (it, n0 + c0), [P, QUARTER], F32)
+                if diagonal(it, n0):
+                    nc.vector.tensor_tensor(out=res[:], in0=signed[it, n0][:, cols], in1=ln[:], op=ALU.max)
+                else:
+                    nc.vector.scalar_tensor_tensor(
+                        out=res[:], in0=acc_of[it, n0][:, cols], scalar=SCORE_SCALE, in1=ln[:], op0=ALU.mult, op1=ALU.max
+                    )
+                nc.sync.dma_start(out=out_rows[P * it : P * (it + 1), n0 + c0 : n0 + c0 + QUARTER], in_=res[:])

@@ -116,15 +116,16 @@ def tile_deepinfomaxlocalglobaljsdmap_kernel(tc, x_bytes, x_scale, y, wu, bu, wg
                     nc.tensor.transpose(bank[:, 2 * r + u, :], words[:, u : 2 * P : 2], ident[:])
             return bank
 
-        def widen_pair(h, a):
-            wide = []
-            for r in (2 * a, 2 * a + 1):
-                row = new("x_wide%d%d" % (h, r), [P, D], BF16)
-                nc.vector.tensor_tensor(
-                    out=row[:], in0=x_raw[h][:, D * r : D * (r + 1)].bitcast(FP8), in1=scale_all[:], op=ALU.mult
-                )
-                wide.append(row)
-            return turn_pair(turn, "turn_bank", wide[0][:], wide[1][:])
+        def widen(h, r):
+            x_wide[h, r] = new("x_wide%d%d" % (h, r), [P, D], BF16)
+            nc.vector.tensor_tensor(
+                out=x_wide[h, r][:], in0=x_raw[h][:, D * r : D * (r + 1)].bitcast(FP8), in1=scale_all[:], op=ALU.mult
+            )
+
+        def turn_x(h, a):
+            return turn_pair(turn, "turn_bank", x_wide[h, 2 * a][:], x_wide[h, 2 * a + 1][:])
+
+        x_wide = {}
 
         x_grouped = [new("x_grouped%d" % h, [P, HALF * PACK], BF16) for h in range(2)]
 
@@ -229,59 +230,73 @@ def tile_deepinfomaxlocalglobaljsdmap_kernel(tc, x_bytes, x_scale, y, wu, bu, wg
             matmul(acc_of[it, n0][:], g_q[g], P * it, u_q[n0, g], 0, n, start=(g == 0), stop=(g == 1))
 
         def flip(it, n0, n):
-            signed[it, n0] = new("signed%d" % n0, [P, n], F32)
-            nc.vector.tensor_tensor(
-                out=signed[it, n0][:], in0=acc_of[it, n0][:], in1=sign[:, n0 % HALF : n0 % HALF + n], op=ALU.mult
-            )
+            signed[it, n0] = new("signed%d_%d" % (it, n0), [P, n], F32)
+            if diagonal(it, n0):
+                nc.vector.tensor_tensor(
+                    out=signed[it, n0][:], in0=acc_of[it, n0][:], in1=sign[:, n0 % HALF : n0 % HALF + n], op=ALU.mult
+                )
+            else:
+                nc.vector.tensor_scalar(
+                    out=signed[it, n0][:], in0=acc_of[it, n0][:], scalar1=SCORE_SCALE, scalar2=None, op0=ALU.mult
+                )
 
         def exp(it, n0, n):
-            e = new("exp%d_%d" % (it, n0), [P, n], F32)
-            if diagonal(it, n0):
-                nc.scalar.activation(out=e[:], in_=signed[it, n0][:], func=ACT.Exp)
-            else:
-                nc.scalar.activation(out=e[:], in_=acc_of[it, n0][:], func=ACT.Exp, scale=SCORE_SCALE)
-            exps[it, n0] = e
+            exps[it, n0] = new("tanh%d_%d" % (it, n0), [P, n], F32)
+            nc.scalar.activation(out=exps[it, n0][:], in_=acc_of[it, n0][:], func=ACT.Tanh, scale=0.5 * SCORE_SCALE)
 
         def cap(it, n0, n):
-            capped[it, n0] = new("capped%d_%d" % (it, n0), [P, n], F32)
-            nc.vector.tensor_scalar(out=capped[it, n0][:], in0=exps[it, n0][:], scalar1=EXP_CAP, scalar2=None, op0=ALU.min)
+            capped[it, n0] = new("abs%d_%d" % (it, n0), [P, n], F32)
+            if n == HALF:
+                nc.scalar.activation(out=capped[it, n0][:], in_=exps[it, n0][:], func=ACT.Abs)
+                return
+            nc.vector.scalar_tensor_tensor(
+                out=capped[it, n0][:], in0=exps[it, n0][:], scalar=-1.0, in1=exps[it, n0][:], op0=ALU.mult, op1=ALU.max
+            )
 
         spread_scale()
         interleave_w(on_vector, "wu", 0, 0)
         interleave_w(on_vector, "wu", 0, 1)
         interleave_w(on_scalar, "wg", 0, 0)
-        b00 = widen_pair(0, 0)
+        widen(0, 0)
+        widen(0, 1)
+        b00 = turn_x(0, 0)
         interleave_w(on_scalar, "wg", 0, 1)
-        b01 = widen_pair(0, 1)
-        by = turn_pair(mm, "mm_bank", y_raw[:, 0:D], y_raw[:, D : 2 * D])
+        widen(0, 2)
+        widen(0, 3)
+        b01 = turn_x(0, 1)
+        by = turn_pair(score, "score_bank", y_raw[:, 0:D], y_raw[:, D : 2 * D])
         wu_q[0] = quantize("wu0", w_grouped["wu", 0])
         empty_x(0, 0, b00)
         empty_x(0, 1, b01)
-        b10 = widen_pair(1, 0)
+        widen(1, 0)
+        widen(1, 1)
+        b10 = turn_x(1, 0)
+        widen(1, 2)
         x_q[0] = quantize("x0", x_grouped[0])
         empty_y(by)
         widen_vectors()
         empty_x(1, 0, b10)
         interleave_w(on_scalar, "wu", 1, 0)
-        pa0 = local_planes(mm, "mm_bank", 0, HALF, 0)
-        b11 = widen_pair(1, 1)
+        interleave_w(on_scalar, "wu", 1, 1)
+        fa0 = fill_direct(mm, "mm_bank", 0, HALF, 0)
+        widen(1, 3)
+        b11 = turn_x(1, 1)
         wg_q[0] = quantize("wg0", w_grouped["wg", 0])
         y_q = quantize("y", y_grouped)
         empty_x(1, 1, b11)
         gp0 = global_gelu(0)
-        interleave_w(on_vector, "wu", 1, 1)
-        interleave_w(on_vector, "wg", 1, 0)
+        ua0 = empty_direct(0, HALF, 0, fa0)
         wu_q[1] = quantize("wu1", w_grouped["wu", 1])
-        interleave_w(on_vector, "wg", 1, 1)
-        ua0 = interleave_planes(0, HALF, 0, pa0)
-        pa1 = local_planes(mm, "mm_bank", 0, HALF, 1)
         x_q[1] = quantize("x1", x_grouped[1])
+        interleave_w(on_scalar, "wg", 1, 0)
+        interleave_w(on_vector, "wg", 1, 1)
+        pa1 = local_planes(mm, "mm_bank", 0, HALF, 1)
+        gg0 = global_gain(0, gp0)
         wg_q[1] = quantize("wg1", w_grouped["wg", 1])
         gp1 = global_gelu(1)
-        gg0 = global_gain(0, gp0)
         u_q[0, 0] = quantize("ua0", ua0)
-        ua1 = interleave_planes(0, HALF, 1, pa1)
         g_q[0] = quantize("g0", gg0)
+        ua1 = interleave_planes(0, HALF, 1, pa1)
         ph0 = local_planes(mm, "mm_bank", HALF, HALF, 0)
         gg1 = global_gain(1, gp1)
         u_q[0, 1] = quantize("ua1", ua1)
@@ -293,39 +308,39 @@ def tile_deepinfomaxlocalglobaljsdmap_kernel(tc, x_bytes, x_scale, y, wu, bu, wg
             scores(it, 0, HALF, 0)
             scores(it, 0, HALF, 1)
         uh0 = interleave_planes(HALF, HALF, 0, ph0)
-        flip(0, 0, HALF)
+        ub1 = interleave_planes(HALF, QUARTER, 1, pb1)
         u_h1 = quantize("uh0", uh0)
         u_q[HALF, 0] = (u_h1[0][:, 0:QUARTER], u_h1[1][:, 0:QUARTER])
         u_q[HALF + QUARTER, 0] = (u_h1[0][:, QUARTER:HALF], u_h1[1][:, QUARTER:HALF])
         for pool, tag, n0 in ((turn, "turn_bank", HALF), (mm, "mm_bank", HALF + QUARTER)):
-            for it in (1, 0):
+            for it in (0, 1):
                 acc_of[it, n0] = pool.tile([P, QUARTER], F32, name=tag)
                 scores(it, n0, QUARTER, 0)
-        ub1 = interleave_planes(HALF, QUARTER, 1, pb1)
+
         uc1 = interleave_planes(HALF + QUARTER, QUARTER, 1, pc1)
         u_q[HALF, 1] = quantize("ub1", ub1)
+
         u_q[HALF + QUARTER, 1] = quantize("uc1", uc1)
         for n0 in (HALF, HALF + QUARTER):
-            for it in (1, 0):
+            for it in (0, 1):
                 scores(it, n0, QUARTER, 1)
-        flip(1, HALF, QUARTER)
-        flip(1, HALF + QUARTER, QUARTER)
         blocks = [(1, 0, HALF), (0, 0, HALF), (0, HALF, QUARTER), (1, HALF, QUARTER), (0, HALF + QUARTER, QUARTER), (1, HALF + QUARTER, QUARTER)]
-        for blk in blocks:
-            exp(*blk)
-        for blk in blocks:
+        for step in (exp, cap):
+            for blk in blocks[:2]:
+                step(*blk)
+        for step in (exp, flip):
+            for blk in blocks[2:] if step is exp else blocks:
+                step(*blk)
+        for blk in blocks[2:]:
             cap(*blk)
         out_rows = out.rearrange("i j l -> i (j l)")
         for it, n0, n in blocks:
             for c0 in range(0, n, QUARTER):
                 cols = slice(c0, c0 + QUARTER)
                 ln = new("ln%d_%d" % (it, n0 + c0), [P, QUARTER], F32)
-                nc.scalar.activation(out=ln[:], in_=capped[it, n0][:, cols], func=ACT.Ln, bias=1.0)
+                nc.scalar.activation(out=ln[:], in_=capped[it, n0][:, cols], func=ACT.Ln, scale=0.5, bias=0.5)
                 res = new("res%d_%d" % (it, n0 + c0), [P, QUARTER], F32)
-                if diagonal(it, n0):
-                    nc.vector.tensor_tensor(out=res[:], in0=signed[it, n0][:, cols], in1=ln[:], op=ALU.max)
-                else:
-                    nc.vector.scalar_tensor_tensor(
-                        out=res[:], in0=acc_of[it, n0][:, cols], scalar=SCORE_SCALE, in1=ln[:], op0=ALU.mult, op1=ALU.max
-                    )
+                nc.vector.scalar_tensor_tensor(
+                    out=res[:], in0=signed[it, n0][:, cols], scalar=0.0, in1=ln[:], op0=ALU.max, op1=ALU.subtract
+                )
                 nc.sync.dma_start(out=out_rows[P * it : P * (it + 1), n0 + c0 : n0 + c0 + QUARTER], in_=res[:])

@@ -20,7 +20,6 @@ PACK = 4
 HALF = 512
 QUARTER = 256
 SCORE_SCALE = 1.0 / 16.0
-EXP_CAP = 2.0 ** 60
 
 
 def tile_deepinfomaxlocalglobaljsdmap_kernel(tc, x_bytes, x_scale, y, wu, bu, wg, bg, gain, out):
@@ -28,12 +27,15 @@ def tile_deepinfomaxlocalglobaljsdmap_kernel(tc, x_bytes, x_scale, y, wu, bu, wg
     with ExitStack() as ctx:
         sb = ctx.enter_context(tc.tile_pool(name="sb", bufs=1))
         turn = ctx.enter_context(tc.psum_pool(name="turn", bufs=2))
-        mm = ctx.enter_context(tc.psum_pool(name="mm", bufs=4))
-        score = ctx.enter_context(tc.psum_pool(name="score", bufs=2))
+        local = ctx.enter_context(tc.psum_pool(name="local", bufs=4))
+        glob = ctx.enter_context(tc.psum_pool(name="glob", bufs=2))
         ctx.enter_context(tc.manual_schedule())
 
         def new(name, shape, dtype):
             return sb.tile(shape, dtype, name=name, align_bytes=64)
+
+        def bank_of(pool, shape):
+            return pool.tile(shape, F32, name="bank")
 
         def quantize(name, grouped):
             width = grouped.shape[1] // PACK
@@ -53,6 +55,12 @@ def tile_deepinfomaxlocalglobaljsdmap_kernel(tc, x_bytes, x_scale, y, wu, bu, wg
                 stop=stop,
             )
 
+        def from_planes(planes, run):
+            return planes[:].rearrange("p t (c i) -> p c t i", i=run)
+
+        def into_grouped(flat, run):
+            return flat.rearrange("p (c i t) -> p c t i", i=run, t=PACK)
+
         warm = new("warm", [P, 2], F32)
         nc.vector.memset(warm[:, 0:1], 0.0)
         nc.scalar.activation(out=warm[:, 1:2], in_=warm[:, 0:1], func=ACT.Gelu)
@@ -60,287 +68,254 @@ def tile_deepinfomaxlocalglobaljsdmap_kernel(tc, x_bytes, x_scale, y, wu, bu, wg
         make_identity(nc, ident[:])
         sign = new("sign", [P, P * L], F32)
         nc.vector.tensor_scalar(
-            out=sign[:].rearrange("p (j l) -> p j l", l=L), in0=ident[:].unsqueeze(2).to_broadcast([P, P, L]),
-            scalar1=-2.0 * SCORE_SCALE, scalar2=SCORE_SCALE, op0=ALU.mult, op1=ALU.add,
+            out=sign[:].rearrange("p (j l) -> p j l", l=L),
+            in0=ident[:].unsqueeze(2).to_broadcast([P, P, L]),
+            scalar1=-2.0 * SCORE_SCALE,
+            scalar2=SCORE_SCALE,
+            op0=ALU.mult,
+            op1=ALU.add,
         )
 
         x_rows = x_bytes.rearrange("j l k -> (j l) k")
+        x_raw, w_raw = {}, {}
 
         def load_x(h):
-            raw = new("x_raw%d" % h, [P, L * D], U8)
-            nc.sync.dma_start(out=raw[:], in_=x_rows[HALF * h : HALF * (h + 1), :].rearrange("(p r) k -> p (r k)", r=L))
-            return raw
+            x_raw[h] = new("x_raw%d" % h, [P, L * D], U8)
+            rows = x_rows[HALF * h : HALF * (h + 1), :]
+            nc.sync.dma_start(out=x_raw[h][:], in_=rows.rearrange("(p r) k -> p (r k)", r=L))
 
-        def load_w(name, w, g, a, halves):
-            width = QUARTER * halves
-            c0 = HALF * g + QUARTER * a
-            raw = new("%s_raw%d%d" % (name, g, a), [P, PACK, width], BF16)
-            nc.sync.dma_start(out=raw[:], in_=w[:, c0 : c0 + width].rearrange("(p j) c -> p j c", j=PACK))
-            for b in range(halves):
-                w_raw[name, g, a + b] = raw[:, :, QUARTER * b : QUARTER * (b + 1)]
+        def load_w(name, w, s, parts):
+            c0 = HALF * s + QUARTER * parts[0]
+            width = QUARTER * len(parts)
+            raw = new("%s_raw%d%d" % (name, s, parts[0]), [P, PACK, width], BF16)
+            nc.sync.dma_start(out=raw[:], in_=w[:, c0 : c0 + width].rearrange("(p t) c -> p t c", t=PACK))
+            for b, part in enumerate(parts):
+                w_raw[name, s, part] = raw[:, :, QUARTER * b : QUARTER * (b + 1)]
 
-        x_raw, wu_raw, wg_raw = {}, {}, {}
-        w_raw = {}
         scale4 = new("scale4", [P, PACK], F32)
         nc.sync.dma_start(out=scale4[:], in_=x_scale.rearrange("a b (p t) -> p (a b t)", t=PACK))
-        load_w("wu", wu, 0, 0, 1)
-        load_w("wu", wu, 0, 1, 1)
-        x_raw[0] = load_x(0)
-        load_w("wg", wg, 0, 0, 1)
-        load_w("wg", wg, 0, 1, 1)
+        load_w("wu", wu, 0, [0])
+        load_w("wu", wu, 0, [1])
+        load_x(0)
+        load_w("wg", wg, 0, [0])
+        load_w("wg", wg, 0, [1])
         y_raw = new("y_raw", [P, 2 * D], BF16)
         nc.sync.dma_start(out=y_raw[:], in_=y.rearrange("(p r) k -> p (r k)", r=2))
-        x_raw[1] = load_x(1)
+        load_x(1)
         vec_raw = []
         for name, vec in (("bu", bu), ("bg", bg), ("gain", gain)):
             raw = new(name + "_raw", [P, 2, PACK], BF16)
-            nc.sync.dma_start(out=raw[:], in_=vec.rearrange("(g p t) -> p g t", g=2, t=PACK))
+            nc.sync.dma_start(out=raw[:], in_=vec.rearrange("(s p t) -> p s t", s=2, t=PACK))
             vec_raw.append(raw)
-        load_w("wu", wu, 1, 0, 2)
-        load_w("wg", wg, 1, 0, 2)
-
-        def by_pairs(planes):
-            return planes[:].rearrange("p t (c i) -> p c t i", i=2)
-
-        def into_pairs(flat):
-            return flat.rearrange("p (c i t) -> p c t i", i=2, t=PACK)
-
-        def per_plane(values, n):
-            return values.unsqueeze(1).unsqueeze(3).to_broadcast([P, n // 2, PACK, 2])
-
-        def turn_pair(pool, tag, first, second):
-            bank = pool.tile([P, PACK, P], F32, name=tag)
-            for r, src in enumerate((first, second)):
-                words = src.bitcast(F32)
-                for u in range(2):
-                    nc.tensor.transpose(bank[:, 2 * r + u, :], words[:, u : 2 * P : 2], ident[:])
-            return bank
-
-        def widen(h, r):
-            x_wide[h, r] = new("x_wide%d%d" % (h, r), [P, D], BF16)
-            nc.vector.tensor_tensor(
-                out=x_wide[h, r][:], in0=x_raw[h][:, D * r : D * (r + 1)].bitcast(FP8), in1=scale_all[:], op=ALU.mult
-            )
-
-        def turn_x(h, a):
-            return turn_pair(turn, "turn_bank", x_wide[h, 2 * a][:], x_wide[h, 2 * a + 1][:])
-
-        x_wide = {}
+        load_w("wu", wu, 1, [0, 1])
+        load_w("wg", wg, 1, [0, 1])
 
         x_grouped = [new("x_grouped%d" % h, [P, HALF * PACK], BF16) for h in range(2)]
-
-        def empty_x(h, a, bank):
-            words = x_grouped[h][:].bitcast(F32).rearrange("p (c i a q) -> p a c q i", i=2, a=2, q=PACK)
-            nc.scalar.copy(out=words[:, a], in_=by_pairs(bank))
-
-        def interleave_w(copy, name, g, a):
-            src = w_raw[name, g, a].rearrange("p j (m t) -> p m j t", t=PACK)
-            dst = w_grouped[name, g][:].rearrange("p (t m j) -> p m j t", t=PACK, j=PACK)
-            copy(out=dst[:, P // 2 * a : P // 2 * (a + 1)], in_=src)
-
-        w_grouped = {(name, g): new("%s_grouped%d" % (name, g), [P, HALF * PACK], BF16) for name in ("wu", "wg") for g in range(2)}
-
-        on_vector, on_scalar = nc.vector.tensor_copy, nc.scalar.copy
-        x_q, wu_q, wg_q, u_q = {}, {}, {}, {}
-
-        def fill_direct(pool, tag, n0, n, g):
-            banks = []
-            for c in range(n // P):
-                acc = pool.tile([P, PACK, P], F32, name=tag)
-                for t in range(PACK):
-                    matmul(acc[:, t, :], wu_q[g], P * t, x_q[n0 // HALF], n0 % HALF + P * c, P)
-                banks.append(acc)
-            return banks
-
-        def empty_direct(n0, n, g, banks):
-            grouped = new("u_grouped%d_%d" % (n0, g), [P, n * PACK], BF16)
-            for c, acc in enumerate(banks):
-                nc.vector.tensor_tensor(
-                    out=into_pairs(grouped[:, HALF * c : HALF * (c + 1)]), in0=by_pairs(acc),
-                    in1=per_plane(vecs[:, g, 0:PACK], P), op=ALU.add,
-                )
-            return grouped
-
-        def local_planes(pool, tag, n0, n, g):
-            planes = new("u_planes%d_%d" % (n0, g), [P, PACK, n], BF16)
-            per_bank = HALF // n
-            for a in range(PACK // per_bank):
-                acc = pool.tile([P, per_bank, n], F32, name=tag)
-                ts = range(per_bank * a, per_bank * (a + 1))
-                for s, t in enumerate(ts):
-                    matmul(acc[:, s, :], wu_q[g], P * t, x_q[n0 // HALF], n0 % HALF, n)
-                for s, t in enumerate(ts):
-                    nc.scalar.activation(out=planes[:, t, :], in_=acc[:, s, :], func=ACT.Identity, bias=vecs[:, g, t : t + 1])
-            return planes
-
-        def interleave(grouped, planes):
-            nc.vector.tensor_copy(
-                out=grouped[:].rearrange("p (c i t) -> p c t i", i=PACK, t=PACK),
-                in_=planes[:].rearrange("p t (c i) -> p c t i", i=PACK),
-            )
-
-        def interleave_planes(n0, n, g, planes):
-            grouped = new("u_grouped%d_%d" % (n0, g), [P, n * PACK], BF16)
-            interleave(grouped, planes)
-            return grouped
-
-        def global_gelu(g):
-            planes = new("g_planes%d" % g, [P, PACK, B], F32)
-            for a in range(2):
-                acc = score.tile([P, 2, B], F32, name="score_bank")
-                for s in range(2):
-                    matmul(acc[:, s, :], wg_q[g], P * (2 * a + s), y_q, 0, B)
-                for s in range(2):
-                    t = 2 * a + s
-                    nc.scalar.activation(
-                        out=planes[:, t, :], in_=acc[:, s, :], func=ACT.Gelu, bias=vecs[:, g, PACK + t : PACK + t + 1]
-                    )
-            return planes
-
-        def global_gain(g, planes):
-            grouped = new("g_grouped%d" % g, [P, B * PACK], BF16)
-            nc.vector.tensor_tensor(
-                out=into_pairs(grouped[:]), in0=by_pairs(planes), in1=per_plane(vecs[:, g, 2 * PACK : 3 * PACK], B), op=ALU.mult
-            )
-            return grouped
-
-        def spread_scale():
-            bank = turn.tile([P, PACK, P], F32, name="turn_bank")
-            for t in range(PACK):
-                nc.tensor.transpose(bank[:, t, :], scale4[:, t : t + 1].to_broadcast([P, P]), ident[:])
-            nc.scalar.copy(out=into_pairs(scale_all[:]), in_=by_pairs(bank))
-
-        def widen_vectors():
-            for v in range(3):
-                nc.scalar.copy(out=vecs[:, :, PACK * v : PACK * (v + 1)], in_=vec_raw[v][:])
-
-        def empty_y(bank):
-            nc.scalar.copy(out=into_pairs(y_grouped[:].bitcast(F32)), in_=by_pairs(bank))
-
+        w_grouped = {
+            (name, s): new("%s_grouped%d" % (name, s), [P, HALF * PACK], BF16) for name in ("wu", "wg") for s in range(2)
+        }
         scale_all = new("scale_all", [P, D], F32)
         vecs = new("vecs", [P, 2, 3 * PACK], F32)
         y_grouped = new("y_grouped", [P, B * PACK], BF16)
-        g_q = {}
-        acc_of, signed, capped, exps = {}, {}, {}, {}
+        x_wide, x_q, w_q, u_q, g_q = {}, {}, {}, {}, {}
 
-        def diagonal(it, n0):
-            return it == n0 // HALF
+        def spread_scale():
+            bank = bank_of(turn, [P, PACK, P])
+            for t in range(PACK):
+                nc.tensor.transpose(bank[:, t, :], scale4[:, t : t + 1].to_broadcast([P, P]), ident[:])
+            nc.scalar.copy(out=into_grouped(scale_all[:], 2), in_=from_planes(bank, 2))
 
-        def scores(it, n0, n, g):
-            matmul(acc_of[it, n0][:], g_q[g], P * it, u_q[n0, g], 0, n, start=(g == 0), stop=(g == 1))
+        def widen_vectors():
+            for v, raw in enumerate(vec_raw):
+                nc.scalar.copy(out=vecs[:, :, PACK * v : PACK * (v + 1)], in_=raw[:])
 
-        def flip(it, n0, n):
-            signed[it, n0] = new("signed%d_%d" % (it, n0), [P, n], F32)
-            if diagonal(it, n0):
-                nc.vector.tensor_tensor(
-                    out=signed[it, n0][:], in0=acc_of[it, n0][:], in1=sign[:, n0 % HALF : n0 % HALF + n], op=ALU.mult
-                )
+        def widen_x(h, r):
+            x_wide[h, r] = new("x_wide%d%d" % (h, r), [P, D], BF16)
+            codes = x_raw[h][:, D * r : D * (r + 1)].bitcast(FP8)
+            nc.vector.tensor_tensor(out=x_wide[h, r][:], in0=codes, in1=scale_all[:], op=ALU.mult)
+
+        def turn_rows(pool, first, second):
+            bank = bank_of(pool, [P, PACK, P])
+            for r, rows in enumerate((first, second)):
+                for v in range(2):
+                    nc.tensor.transpose(bank[:, 2 * r + v, :], rows.bitcast(F32)[:, v : 2 * P : 2], ident[:])
+            return bank
+
+        def turn_x(h, a):
+            return turn_rows(turn, x_wide[h, 2 * a][:], x_wide[h, 2 * a + 1][:])
+
+        def empty_x(h, a, bank):
+            words = x_grouped[h][:].bitcast(F32).rearrange("p (c i a q) -> p a c q i", i=2, a=2, q=PACK)
+            nc.scalar.copy(out=words[:, a], in_=from_planes(bank, 2))
+
+        def empty_y(bank):
+            nc.scalar.copy(out=into_grouped(y_grouped[:].bitcast(F32), 2), in_=from_planes(bank, 2))
+
+        def group_w(copy, name, s, part):
+            src = w_raw[name, s, part].rearrange("p j (m t) -> p m j t", t=PACK)
+            dst = w_grouped[name, s][:].rearrange("p (t m j) -> p m j t", t=PACK, j=PACK)
+            copy(out=dst[:, P // 2 * part : P // 2 * (part + 1)], in_=src)
+
+        def quantize_w(name, s):
+            w_q[name, s] = quantize("%s%d" % (name, s), w_grouped[name, s])
+
+        def local_planes(pool, n0, n, s):
+            planes = new("u_planes%d_%d" % (n0, s), [P, PACK, n], BF16)
+            per_bank = HALF // n
+            for t0 in range(0, PACK, per_bank):
+                bank = bank_of(pool, [P, per_bank, n])
+                for b in range(per_bank):
+                    matmul(bank[:, b, :], w_q["wu", s], P * (t0 + b), x_q[n0 // HALF], n0 % HALF, n)
+                for b in range(per_bank):
+                    t = t0 + b
+                    nc.scalar.activation(
+                        out=planes[:, t, :], in_=bank[:, b, :], func=ACT.Identity, bias=vecs[:, s, t : t + 1]
+                    )
+            return planes
+
+        def group_u(n0, n, s, planes):
+            grouped = new("u_grouped%d_%d" % (n0, s), [P, n * PACK], BF16)
+            nc.vector.tensor_copy(out=into_grouped(grouped[:], PACK), in_=from_planes(planes, PACK))
+            return grouped
+
+        def global_planes(s):
+            planes = new("g_planes%d" % s, [P, PACK, B], F32)
+            for t0 in range(0, PACK, 2):
+                bank = bank_of(glob, [P, 2, B])
+                for b in range(2):
+                    matmul(bank[:, b, :], w_q["wg", s], P * (t0 + b), y_q, 0, B)
+                for b in range(2):
+                    t = t0 + b
+                    nc.scalar.activation(
+                        out=planes[:, t, :], in_=bank[:, b, :], func=ACT.Gelu, bias=vecs[:, s, PACK + t : PACK + t + 1]
+                    )
+            return planes
+
+        def group_g(s, planes):
+            grouped = new("g_grouped%d" % s, [P, B * PACK], BF16)
+            gains = vecs[:, s, 2 * PACK : 3 * PACK].unsqueeze(1).unsqueeze(3).to_broadcast([P, B // 2, PACK, 2])
+            nc.vector.tensor_tensor(out=into_grouped(grouped[:], 2), in0=from_planes(planes, 2), in1=gains, op=ALU.mult)
+            return grouped
+
+        acc, signed, tanh, size = {}, {}, {}, {}
+
+        def scores(block, s):
+            it, n0, n = block
+            matmul(acc[block][:], g_q[s], P * it, u_q[n0, s], 0, n, start=(s == 0), stop=(s == 1))
+
+        def take_signed(block):
+            it, n0, n = block
+            signed[block] = new("signed%d_%d" % (it, n0), [P, n], F32)
+            if it == n0 // HALF:
+                flips = sign[:, n0 % HALF : n0 % HALF + n]
+                nc.vector.tensor_tensor(out=signed[block][:], in0=acc[block][:], in1=flips, op=ALU.mult)
             else:
                 nc.vector.tensor_scalar(
-                    out=signed[it, n0][:], in0=acc_of[it, n0][:], scalar1=SCORE_SCALE, scalar2=None, op0=ALU.mult
+                    out=signed[block][:], in0=acc[block][:], scalar1=SCORE_SCALE, scalar2=None, op0=ALU.mult
                 )
 
-        def exp(it, n0, n):
-            exps[it, n0] = new("tanh%d_%d" % (it, n0), [P, n], F32)
-            nc.scalar.activation(out=exps[it, n0][:], in_=acc_of[it, n0][:], func=ACT.Tanh, scale=0.5 * SCORE_SCALE)
+        def take_tanh(block):
+            it, n0, n = block
+            tanh[block] = new("tanh%d_%d" % (it, n0), [P, n], F32)
+            size[block] = new("size%d_%d" % (it, n0), [P, n], F32)
+            nc.scalar.activation(out=tanh[block][:], in_=acc[block][:], func=ACT.Tanh, scale=0.5 * SCORE_SCALE)
 
-        def cap(it, n0, n):
-            capped[it, n0] = new("abs%d_%d" % (it, n0), [P, n], F32)
-            if n == HALF:
-                nc.scalar.activation(out=capped[it, n0][:], in_=exps[it, n0][:], func=ACT.Abs)
-                return
-            nc.vector.scalar_tensor_tensor(
-                out=capped[it, n0][:], in0=exps[it, n0][:], scalar=-1.0, in1=exps[it, n0][:], op0=ALU.mult, op1=ALU.max
-            )
+        on_vector, on_scalar = nc.vector.tensor_copy, nc.scalar.copy
 
         spread_scale()
-        interleave_w(on_vector, "wu", 0, 0)
-        interleave_w(on_vector, "wu", 0, 1)
-        interleave_w(on_scalar, "wg", 0, 0)
-        widen(0, 0)
-        widen(0, 1)
-        b00 = turn_x(0, 0)
-        interleave_w(on_scalar, "wg", 0, 1)
-        widen(0, 2)
-        widen(0, 3)
-        b01 = turn_x(0, 1)
-        by = turn_pair(score, "score_bank", y_raw[:, 0:D], y_raw[:, D : 2 * D])
-        wu_q[0] = quantize("wu0", w_grouped["wu", 0])
-        empty_x(0, 0, b00)
-        empty_x(0, 1, b01)
-        widen(1, 0)
-        widen(1, 1)
-        b10 = turn_x(1, 0)
-        widen(1, 2)
+        group_w(on_vector, "wu", 0, 0)
+        group_w(on_vector, "wu", 0, 1)
+        x_banks = []
+        for a in range(2):
+            group_w(on_scalar, "wg", 0, a)
+            widen_x(0, 2 * a)
+            widen_x(0, 2 * a + 1)
+            x_banks.append(turn_x(0, a))
+        y_bank = turn_rows(local, y_raw[:, 0:D], y_raw[:, D : 2 * D])
+        quantize_w("wu", 0)
+        for a in range(2):
+            empty_x(0, a, x_banks[a])
+
+        widen_x(1, 0)
+        widen_x(1, 1)
+        x_bank = turn_x(1, 0)
+        widen_x(1, 2)
         x_q[0] = quantize("x0", x_grouped[0])
-        empty_y(by)
+        empty_y(y_bank)
         widen_vectors()
-        empty_x(1, 0, b10)
-        interleave_w(on_scalar, "wu", 1, 0)
-        interleave_w(on_scalar, "wu", 1, 1)
-        fa0 = fill_direct(mm, "mm_bank", 0, HALF, 0)
-        widen(1, 3)
-        b11 = turn_x(1, 1)
-        wg_q[0] = quantize("wg0", w_grouped["wg", 0])
+        empty_x(1, 0, x_bank)
+        group_w(on_scalar, "wu", 1, 0)
+        u_planes = local_planes(local, 0, HALF, 0)
+        widen_x(1, 3)
+        x_bank = turn_x(1, 1)
+        quantize_w("wg", 0)
         y_q = quantize("y", y_grouped)
-        empty_x(1, 1, b11)
-        gp0 = global_gelu(0)
-        ua0 = empty_direct(0, HALF, 0, fa0)
-        wu_q[1] = quantize("wu1", w_grouped["wu", 1])
+        empty_x(1, 1, x_bank)
+        g_planes = [global_planes(0)]
+
+        group_w(on_vector, "wu", 1, 1)
+        group_w(on_vector, "wg", 1, 0)
+        quantize_w("wu", 1)
+        group_w(on_vector, "wg", 1, 1)
+        u_grouped = group_u(0, HALF, 0, u_planes)
+        u_planes = local_planes(local, 0, HALF, 1)
         x_q[1] = quantize("x1", x_grouped[1])
-        interleave_w(on_scalar, "wg", 1, 0)
-        interleave_w(on_vector, "wg", 1, 1)
-        pa1 = local_planes(mm, "mm_bank", 0, HALF, 1)
-        gg0 = global_gain(0, gp0)
-        wg_q[1] = quantize("wg1", w_grouped["wg", 1])
-        gp1 = global_gelu(1)
-        u_q[0, 0] = quantize("ua0", ua0)
-        g_q[0] = quantize("g0", gg0)
-        ua1 = interleave_planes(0, HALF, 1, pa1)
-        ph0 = local_planes(mm, "mm_bank", HALF, HALF, 0)
-        gg1 = global_gain(1, gp1)
-        u_q[0, 1] = quantize("ua1", ua1)
-        g_q[1] = quantize("g1", gg1)
-        pb1 = local_planes(turn, "turn_bank", HALF, QUARTER, 1)
-        pc1 = local_planes(mm, "mm_bank", HALF + QUARTER, QUARTER, 1)
-        for it in (0, 1):
-            acc_of[it, 0] = score.tile([P, HALF], F32, name="score_bank")
-            scores(it, 0, HALF, 0)
-            scores(it, 0, HALF, 1)
-        uh0 = interleave_planes(HALF, HALF, 0, ph0)
-        ub1 = interleave_planes(HALF, QUARTER, 1, pb1)
-        u_h1 = quantize("uh0", uh0)
-        u_q[HALF, 0] = (u_h1[0][:, 0:QUARTER], u_h1[1][:, 0:QUARTER])
-        u_q[HALF + QUARTER, 0] = (u_h1[0][:, QUARTER:HALF], u_h1[1][:, QUARTER:HALF])
-        for pool, tag, n0 in ((turn, "turn_bank", HALF), (mm, "mm_bank", HALF + QUARTER)):
-            for it in (0, 1):
-                acc_of[it, n0] = pool.tile([P, QUARTER], F32, name=tag)
-                scores(it, n0, QUARTER, 0)
+        quantize_w("wg", 1)
+        g_planes.append(global_planes(1))
+        g_grouped = group_g(0, g_planes[0])
+        u_q[0, 0] = quantize("u_first0", u_grouped)
+        u_grouped = group_u(0, HALF, 1, u_planes)
+        g_q[0] = quantize("g0", g_grouped)
+        u_planes = local_planes(local, HALF, HALF, 0)
+        g_grouped = group_g(1, g_planes[1])
+        u_q[0, 1] = quantize("u_first1", u_grouped)
+        g_q[1] = quantize("g1", g_grouped)
 
-        uc1 = interleave_planes(HALF + QUARTER, QUARTER, 1, pc1)
-        u_q[HALF, 1] = quantize("ub1", ub1)
+        third, fourth = HALF, HALF + QUARTER
+        third_planes = local_planes(turn, third, QUARTER, 1)
+        fourth_planes = local_planes(local, fourth, QUARTER, 1)
+        early = [(1, 0, HALF), (0, 0, HALF)]
+        late = [(it, n0, QUARTER) for n0 in (third, fourth) for it in range(2)]
+        for block in reversed(early):
+            acc[block] = bank_of(glob, [P, HALF])
+            scores(block, 0)
+            scores(block, 1)
+        u_grouped = group_u(HALF, HALF, 0, u_planes)
+        third_grouped = group_u(third, QUARTER, 1, third_planes)
+        codes, scales = quantize("u_second0", u_grouped)
+        for n0 in (third, fourth):
+            cols = slice(n0 - HALF, n0 - HALF + QUARTER)
+            u_q[n0, 0] = (codes[:, cols], scales[:, cols])
+        for block in late:
+            acc[block] = bank_of(turn if block[1] == third else local, [P, QUARTER])
+            scores(block, 0)
+        fourth_grouped = group_u(fourth, QUARTER, 1, fourth_planes)
+        u_q[third, 1] = quantize("u_third1", third_grouped)
+        u_q[fourth, 1] = quantize("u_fourth1", fourth_grouped)
+        for block in late:
+            scores(block, 1)
 
-        u_q[HALF + QUARTER, 1] = quantize("uc1", uc1)
-        for n0 in (HALF, HALF + QUARTER):
-            for it in (0, 1):
-                scores(it, n0, QUARTER, 1)
-        blocks = [(1, 0, HALF), (0, 0, HALF), (0, HALF, QUARTER), (1, HALF, QUARTER), (0, HALF + QUARTER, QUARTER), (1, HALF + QUARTER, QUARTER)]
-        for step in (exp, cap):
-            for blk in blocks[:2]:
-                step(*blk)
-        for step in (exp, flip):
-            for blk in blocks[2:] if step is exp else blocks:
-                step(*blk)
-        for blk in blocks[2:]:
-            cap(*blk)
+        for block in early:
+            take_tanh(block)
+        for block in early:
+            nc.scalar.activation(out=size[block][:], in_=tanh[block][:], func=ACT.Abs)
+        for block in late:
+            take_tanh(block)
+        for block in early + late:
+            take_signed(block)
+        for block in late:
+            nc.vector.scalar_tensor_tensor(
+                out=size[block][:], in0=tanh[block][:], scalar=-1.0, in1=tanh[block][:], op0=ALU.mult, op1=ALU.max
+            )
         out_rows = out.rearrange("i j l -> i (j l)")
-        for it, n0, n in blocks:
+        for block in early + late:
+            it, n0, n = block
             for c0 in range(0, n, QUARTER):
                 cols = slice(c0, c0 + QUARTER)
-                ln = new("ln%d_%d" % (it, n0 + c0), [P, QUARTER], F32)
-                nc.scalar.activation(out=ln[:], in_=capped[it, n0][:, cols], func=ACT.Ln, scale=0.5, bias=0.5)
+                log = new("log%d_%d" % (it, n0 + c0), [P, QUARTER], F32)
+                nc.scalar.activation(out=log[:], in_=size[block][:, cols], func=ACT.Ln, scale=0.5, bias=0.5)
                 res = new("res%d_%d" % (it, n0 + c0), [P, QUARTER], F32)
                 nc.vector.scalar_tensor_tensor(
-                    out=res[:], in0=signed[it, n0][:, cols], scalar=0.0, in1=ln[:], op0=ALU.max, op1=ALU.subtract
+                    out=res[:], in0=signed[block][:, cols], scalar=0.0, in1=log[:], op0=ALU.max, op1=ALU.subtract
                 )
                 nc.sync.dma_start(out=out_rows[P * it : P * (it + 1), n0 + c0 : n0 + c0 + QUARTER], in_=res[:])

from contextlib import ExitStack

import concourse.mybir as mybir
from concourse.masks import make_identity

B, L, D, E = 256, 4, 512, 1024
FLOPS = 2 * (B * L * D * E + B * D * E + B * B * L * E)

F32 = mybir.dt.float32
BF16 = mybir.dt.bfloat16
U32 = mybir.dt.uint32
U8 = mybir.dt.uint8
FP8 = mybir.dt.float8_e4m3fn
FP8X4 = mybir.dt.float8_e4m3fn_x4
ALU = mybir.AluOpType
ACT = mybir.ActivationFunctionType

P = 128
PACK = 4
HALF = 512
QUARTER = 256
SCORE_SCALE = 1.0 / 16.0


def tile_deepinfomaxlocalglobaljsdmap_kernel(tc, x_bytes, x_scale, y, wu, bu, wg, bg, gain, out):
    nc = tc.nc
    with ExitStack() as ctx:
        sb = ctx.enter_context(tc.tile_pool(name="sb", bufs=1))
        turn = ctx.enter_context(tc.psum_pool(name="turn", bufs=2))
        local = ctx.enter_context(tc.psum_pool(name="local", bufs=4))
        glob = ctx.enter_context(tc.psum_pool(name="glob", bufs=2))
        ctx.enter_context(tc.manual_schedule())

        def new(name, shape, dtype):
            return sb.tile(shape, dtype, name=name, align_bytes=64)

        def bank_of(pool, shape):
            return pool.tile(shape, F32, name="bank")

        def quantize(name, grouped):
            width = grouped.shape[1] // PACK
            codes = new(name + "_codes", [P, width], U32)
            scales = new(name + "_scales", [P, width], U8)
            nc.vector.quantize_mx(out=codes[:].bitcast(FP8X4), scales=scales[:], in_=grouped[:])
            return codes, scales

        def matmul(acc, stationary, m0, moving, n0, n, start=True, stop=True):
            nc.tensor.matmul_mx(
                out=acc,
                lhsT=stationary[0][:, m0 : m0 + P].bitcast(FP8X4),
                lhsT_scale=stationary[1][:, m0 : m0 + P],
                rhs=moving[0][:, n0 : n0 + n].bitcast(FP8X4),
                rhs_scale=moving[1][:, n0 : n0 + n],
                start=start,
                stop=stop,
            )

        def from_planes(planes, run):
            return planes[:].rearrange("p t (c i) -> p c t i", i=run)

        def into_grouped(flat, run):
            return flat.rearrange("p (c i t) -> p c t i", i=run, t=PACK)

        warm = new("warm", [P, 2], F32)
        nc.vector.memset(warm[:, 0:1], 0.0)
        nc.scalar.activation(out=warm[:, 1:2], in_=warm[:, 0:1], func=ACT.Gelu)
        ident = new("ident", [P, P], F32)
        make_identity(nc, ident[:])
        sign = new("sign", [P, P * L], F32)
        nc.vector.tensor_scalar(
            out=sign[:].rearrange("p (j l) -> p j l", l=L),
            in0=ident[:].unsqueeze(2).to_broadcast([P, P, L]),
            scalar1=-2.0 * SCORE_SCALE,
            scalar2=SCORE_SCALE,
            op0=ALU.mult,
            op1=ALU.add,
        )

        x_rows = x_bytes.rearrange("j l k -> (j l) k")
        x_raw, w_raw = {}, {}

        def load_x(h):
            x_raw[h] = new("x_raw%d" % h, [P, L * D], U8)
            rows = x_rows[HALF * h : HALF * (h + 1), :]
            nc.sync.dma_start(out=x_raw[h][:], in_=rows.rearrange("(p r) k -> p (r k)", r=L))

        def load_w(name, w, s, parts):
            c0 = HALF * s + QUARTER * parts[0]
            width = QUARTER * len(parts)
            raw = new("%s_raw%d%d" % (name, s, parts[0]), [P, PACK, width], BF16)
            nc.sync.dma_start(out=raw[:], in_=w[:, c0 : c0 + width].rearrange("(p t) c -> p t c", t=PACK))
            for b, part in enumerate(parts):
                w_raw[name, s, part] = raw[:, :, QUARTER * b : QUARTER * (b + 1)]

        scale4 = new("scale4", [P, PACK], F32)
        nc.sync.dma_start(out=scale4[:], in_=x_scale.rearrange("a b (p t) -> p (a b t)", t=PACK))
        load_w("wu", wu, 0, [0])
        load_w("wu", wu, 0, [1])
        load_x(0)
        load_w("wg", wg, 0, [0])
        load_w("wg", wg, 0, [1])
        y_raw = new("y_raw", [P, 2 * D], BF16)
        nc.sync.dma_start(out=y_raw[:], in_=y.rearrange("(p r) k -> p (r k)", r=2))
        load_x(1)
        vec_raw = []
        for name, vec in (("bu", bu), ("bg", bg), ("gain", gain)):
            raw = new(name + "_raw", [P, 2, PACK], BF16)
            nc.sync.dma_start(out=raw[:], in_=vec.rearrange("(s p t) -> p s t", s=2, t=PACK))
            vec_raw.append(raw)
        load_w("wu", wu, 1, [0, 1])
        load_w("wg", wg, 1, [0, 1])

        x_grouped = [new("x_grouped%d" % h, [P, HALF * PACK], BF16) for h in range(2)]
        w_grouped = {
            (name, s): new("%s_grouped%d" % (name, s), [P, HALF * PACK], BF16) for name in ("wu", "wg") for s in range(2)
        }
        scale_all = new("scale_all", [P, D], F32)
        vecs = new("vecs", [P, 2, 3 * PACK], F32)
        y_grouped = new("y_grouped", [P, B * PACK], BF16)
        x_wide, x_q, w_q, u_q, g_q = {}, {}, {}, {}, {}

        def spread_scale():
            bank = bank_of(turn, [P, PACK, P])
            for t in range(PACK):
                nc.tensor.transpose(bank[:, t, :], scale4[:, t : t + 1].to_broadcast([P, P]), ident[:])
            nc.scalar.copy(out=into_grouped(scale_all[:], 2), in_=from_planes(bank, 2))

        def widen_vectors():
            for v, raw in enumerate(vec_raw):
                nc.scalar.copy(out=vecs[:, :, PACK * v : PACK * (v + 1)], in_=raw[:])

        def widen_x(h, r):
            x_wide[h, r] = new("x_wide%d%d" % (h, r), [P, D], BF16)
            codes = x_raw[h][:, D * r : D * (r + 1)].bitcast(FP8)
            nc.vector.tensor_tensor(out=x_wide[h, r][:], in0=codes, in1=scale_all[:], op=ALU.mult)

        def turn_rows(pool, first, second):
            bank = bank_of(pool, [P, PACK, P])
            for r, rows in enumerate((first, second)):
                for v in range(2):
                    nc.tensor.transpose(bank[:, 2 * r + v, :], rows.bitcast(F32)[:, v : 2 * P : 2], ident[:])
            return bank

        def turn_x(h, a):
            return turn_rows(turn, x_wide[h, 2 * a][:], x_wide[h, 2 * a + 1][:])

        def empty_x(h, a, bank):
            words = x_grouped[h][:].bitcast(F32).rearrange("p (c i a q) -> p a c q i", i=2, a=2, q=PACK)
            nc.scalar.copy(out=words[:, a], in_=from_planes(bank, 2))

        def empty_y(bank):
            nc.scalar.copy(out=into_grouped(y_grouped[:].bitcast(F32), 2), in_=from_planes(bank, 2))

        def group_w(copy, name, s, part):
            src = w_raw[name, s, part].rearrange("p j (m t) -> p m j t", t=PACK)
            dst = w_grouped[name, s][:].rearrange("p (t m j) -> p m j t", t=PACK, j=PACK)
            copy(out=dst[:, P // 2 * part : P // 2 * (part + 1)], in_=src)

        def quantize_w(name, s):
            w_q[name, s] = quantize("%s%d" % (name, s), w_grouped[name, s])

        def local_planes(pool, n0, n, s):
            planes = new("u_planes%d_%d" % (n0, s), [P, PACK, n], BF16)
            per_bank = HALF // n
            for t0 in range(0, PACK, per_bank):
                bank = bank_of(pool, [P, per_bank, n])
                for b in range(per_bank):
                    matmul(bank[:, b, :], w_q["wu", s], P * (t0 + b), x_q[n0 // HALF], n0 % HALF, n)
                for b in range(per_bank):
                    t = t0 + b
                    nc.scalar.activation(
                        out=planes[:, t, :], in_=bank[:, b, :], func=ACT.Identity, bias=vecs[:, s, t : t + 1]
                    )
            return planes

        def group_u(n0, n, s, planes):
            grouped = new("u_grouped%d_%d" % (n0, s), [P, n * PACK], BF16)
            nc.vector.tensor_copy(out=into_grouped(grouped[:], PACK), in_=from_planes(planes, PACK))
            return grouped

        def global_planes(s):
            planes = new("g_planes%d" % s, [P, PACK, B], F32)
            for t0 in range(0, PACK, 2):
                bank = bank_of(glob, [P, 2, B])
                for b in range(2):
                    matmul(bank[:, b, :], w_q["wg", s], P * (t0 + b), y_q, 0, B)
                for b in range(2):
                    t = t0 + b
                    nc.scalar.activation(
                        out=planes[:, t, :], in_=bank[:, b, :], func=ACT.Gelu, bias=vecs[:, s, PACK + t : PACK + t + 1]
                    )
            return planes

        def group_g(s, planes):
            grouped = new("g_grouped%d" % s, [P, B * PACK], BF16)
            gains = vecs[:, s, 2 * PACK : 3 * PACK].unsqueeze(1).unsqueeze(3).to_broadcast([P, B // 2, PACK, 2])
            nc.vector.tensor_tensor(out=into_grouped(grouped[:], 2), in0=from_planes(planes, 2), in1=gains, op=ALU.mult)
            return grouped

        acc, signed, tanh, size = {}, {}, {}, {}

        def scores(block, s):
            it, n0, n = block
            matmul(acc[block][:], g_q[s], P * it, u_q[n0, s], 0, n, start=(s == 0), stop=(s == 1))

        def take_signed(block):
            it, n0, n = block
            signed[block] = new("signed%d_%d" % (it, n0), [P, n], F32)
            if it == n0 // HALF:
                flips = sign[:, n0 % HALF : n0 % HALF + n]
                nc.vector.tensor_tensor(out=signed[block][:], in0=acc[block][:], in1=flips, op=ALU.mult)
            else:
                nc.vector.tensor_scalar(
                    out=signed[block][:], in0=acc[block][:], scalar1=SCORE_SCALE, scalar2=None, op0=ALU.mult
                )

        def take_tanh(block):
            it, n0, n = block
            tanh[block] = new("tanh%d_%d" % (it, n0), [P, n], F32)
            size[block] = new("size%d_%d" % (it, n0), [P, n], F32)
            nc.scalar.activation(out=tanh[block][:], in_=acc[block][:], func=ACT.Tanh, scale=0.5 * SCORE_SCALE)

        on_vector, on_scalar = nc.vector.tensor_copy, nc.scalar.copy

        spread_scale()
        group_w(on_vector, "wu", 0, 0)
        group_w(on_vector, "wu", 0, 1)
        x_banks = []
        for a in range(2):
            group_w(on_scalar, "wg", 0, a)
            widen_x(0, 2 * a)
            widen_x(0, 2 * a + 1)
            x_banks.append(turn_x(0, a))
        y_bank = turn_rows(local, y_raw[:, 0:D], y_raw[:, D : 2 * D])
        quantize_w("wu", 0)
        for a in range(2):
            empty_x(0, a, x_banks[a])

        widen_x(1, 0)
        widen_x(1, 1)
        x_bank = turn_x(1, 0)
        widen_x(1, 2)
        x_q[0] = quantize("x0", x_grouped[0])
        empty_y(y_bank)
        widen_vectors()
        empty_x(1, 0, x_bank)
        group_w(on_scalar, "wu", 1, 0)
        u_planes = local_planes(local, 0, HALF, 0)
        widen_x(1, 3)
        x_bank = turn_x(1, 1)
        quantize_w("wg", 0)
        y_q = quantize("y", y_grouped)
        empty_x(1, 1, x_bank)
        g_planes = [global_planes(0)]

        group_w(on_vector, "wu", 1, 1)
        group_w(on_vector, "wg", 1, 0)
        quantize_w("wu", 1)
        group_w(on_vector, "wg", 1, 1)
        u_grouped = group_u(0, HALF, 0, u_planes)
        u_planes = local_planes(local, 0, HALF, 1)
        x_q[1] = quantize("x1", x_grouped[1])
        quantize_w("wg", 1)
        g_planes.append(global_planes(1))
        g_grouped = group_g(0, g_planes[0])
        u_q[0, 0] = quantize("u_first0", u_grouped)
        u_grouped = group_u(0, HALF, 1, u_planes)
        g_q[0] = quantize("g0", g_grouped)
        u_planes = local_planes(local, HALF, HALF, 0)
        g_grouped = group_g(1, g_planes[1])
        u_q[0, 1] = quantize("u_first1", u_grouped)
        g_q[1] = quantize("g1", g_grouped)

        third, fourth = HALF, HALF + QUARTER
        third_planes = local_planes(turn, third, QUARTER, 1)
        fourth_planes = local_planes(local, fourth, QUARTER, 1)
        early = [(1, 0, HALF), (0, 0, HALF)]
        late = [(it, n0, QUARTER) for n0 in (third, fourth) for it in range(2)]
        for block in reversed(early):
            acc[block] = bank_of(glob, [P, HALF])
            scores(block, 0)
            scores(block, 1)
        u_grouped = group_u(HALF, HALF, 0, u_planes)
        third_grouped = group_u(third, QUARTER, 1, third_planes)
        codes, scales = quantize("u_second0", u_grouped)
        for n0 in (third, fourth):
            cols = slice(n0 - HALF, n0 - HALF + QUARTER)
            u_q[n0, 0] = (codes[:, cols], scales[:, cols])
        for block in late:
            acc[block] = bank_of(turn if block[1] == third else local, [P, QUARTER])
            scores(block, 0)
        fourth_grouped = group_u(fourth, QUARTER, 1, fourth_planes)
        u_q[third, 1] = quantize("u_third1", third_grouped)
        u_q[fourth, 1] = quantize("u_fourth1", fourth_grouped)
        for block in late:
            scores(block, 1)

        for block in early:
            take_tanh(block)
        for block in early:
            nc.scalar.activation(out=size[block][:], in_=tanh[block][:], func=ACT.Abs)
        for block in late:
            take_tanh(block)
        for block in early + late:
            take_signed(block)
        for block in late:
            nc.vector.scalar_tensor_tensor(
                out=size[block][:], in0=tanh[block][:], scalar=-1.0, in1=tanh[block][:], op0=ALU.mult, op1=ALU.max
            )
        out_rows = out.rearrange("i j l -> i (j l)")
        for block in early + late:
            it, n0, n = block
            for c0 in range(0, n, QUARTER):
                cols = slice(c0, c0 + QUARTER)
                log = new("log%d_%d" % (it, n0 + c0), [P, QUARTER], F32)
                nc.scalar.activation(out=log[:], in_=size[block][:, cols], func=ACT.Ln, scale=0.5, bias=0.5)
                res = new("res%d_%d" % (it, n0 + c0), [P, QUARTER], F32)
                nc.vector.scalar_tensor_tensor(
                    out=res[:], in0=signed[block][:, cols], scalar=0.0, in1=log[:], op0=ALU.max, op1=ALU.subtract
                )
                nc.sync.dma_start(out=out_rows[P * it : P * (it + 1), n0 + c0 : n0 + c0 + QUARTER], in_=res[:])
